import numpy as np
import ml_dtypes


def mxq(x, axis, fmt="e4m3"):
    dtype, down = {"e4m3": (ml_dtypes.float8_e4m3fn, 7), "e5m2": (ml_dtypes.float8_e5m2, 14)}[fmt]
    v = np.moveaxis(np.asarray(x, np.float32).astype(ml_dtypes.bfloat16).astype(np.float64), axis, -1)
    blocks = v.reshape(v.shape[:-1] + (-1, 32))
    amax = np.abs(blocks).max(-1, keepdims=True)
    byte = np.maximum(np.where(amax > 0, np.frexp(amax)[1] - 1 + 127, 0) - down, 1)
    scale = np.exp2(byte - 127.0)
    codes = (blocks / scale).astype(np.float32).astype(dtype).astype(np.float64)
    return np.moveaxis((codes * scale).reshape(v.shape), -1, axis)


WIDE = False


def mx_kscale(k):
    if not WIDE:
        return np.ones(k)
    levels = np.array([10, -10, 5, -5, 0])
    if k % 512:
        return np.exp2(np.random.permutation(np.resize(levels, k // 32))).repeat(32)
    a = np.empty((k // 512, 16))
    for p in range(k // 512):
        a[p, :8] = np.random.permutation(np.resize(levels, 8))
        for g in range(8):
            far = levels[np.abs(levels - a[p, g]) >= 10]
            a[p, g + 8] = far[np.random.randint(len(far))]
    return np.exp2(a.ravel()).repeat(32)


def f64(x):
    return np.asarray(x).astype(np.float64)


def striped(idx):
    return np.tile(idx.reshape(-1, 16).T, (8, 1)).astype(np.uint16)


def unstriped(offs):
    return offs[:16].T.reshape(-1).astype(np.int64)


def relu(v):
    return np.maximum(v, 0.0)


K, T, D, S, V, H, N = 512, 2048, 4, 768, 384, 512, 256


def setup_inputs():
    n = np.random.standard_normal
    s = mx_kscale(K)[:, None]
    u = mx_kscale(H)
    return {
        "xT": (n((K, T)) * s).astype(np.float32),
        "w1": (n((K, H)) / np.sqrt(K) / s * u).astype(np.float32),
        "w2": (n((H, N)) / np.sqrt(H) / u[:, None]).astype(np.float32),
        "gate": np.tile(np.random.uniform(0.2, 1.0, (D, 1, V)) / np.sqrt(D), (1, N, 1)).astype(np.float32),
        "offs": striped(np.random.permutation(T)[:S]),
        "pos1": striped(np.random.permutation(S)[:V]),
        "pos2": striped(np.random.permutation(S)[:V]),
        "pos3": striped(np.random.permutation(S)[:V]),
        "pos4": striped(np.random.permutation(S)[:V]),
    }


def reference(xT, w1, w2, gate, offs, pos1, pos2, pos3, pos4):
    idx = unstriped(offs)
    xq = mxq(f64(xT)[:, idx], 0, "e4m3")
    h = relu(mxq(f64(w1), 0, "e4m3").T @ xq)
    y = mxq(f64(w2), 0, "e4m3").T @ mxq(h, 0, "e4m3")
    return sum(f64(gate[d]) * y[:, unstriped(p)] for d, p in enumerate((pos1, pos2, pos3, pos4)))

@@ -1,0 +1,212 @@
+from contextlib import ExitStack
+
+import concourse.mybir as mybir
+
+K, T, D, S, V, H, N = 512, 2048, 4, 768, 384, 512, 256
+FLOPS = 2 * S * (K * H + H * N)
+
+F32 = mybir.dt.float32
+BF16 = mybir.dt.bfloat16
+U32 = mybir.dt.uint32
+U16 = mybir.dt.uint16
+U8 = mybir.dt.uint8
+FP8X4 = mybir.dt.float8_e4m3fn_x4
+ADD, MULT = mybir.AluOpType.add, mybir.AluOpType.mult
+RELU = mybir.ActivationFunctionType.Relu
+
+P = 128
+PACK = 4
+SLICE = 256
+SLICES = S // SLICE
+LANE = 16
+
+
+def tile_picked_sub_mlp_relu_sub_e_kernel(tc, xT, w1, w2, gate, offs, pos1, pos2, pos3, pos4, out):
+    nc = tc.nc
+    with ExitStack() as ctx:
+        keep = ctx.enter_context(tc.tile_pool(name="keep", bufs=1))
+        psum = ctx.enter_context(tc.psum_pool(name="psum", bufs=1))
+
+        def sb(shape, dtype, name):
+            return keep.tile(shape, dtype, name=name, align_bytes=64)
+
+        offs_sb = keep.tile([P, S // LANE], U16, name="offs_sb")
+        pos_sb = [keep.tile([P, V // LANE], U16, name=f"pos_sb{d}") for d in range(D)]
+
+        x_raw = [sb([P, T], F32, f"x_raw{j}") for j in range(PACK)]
+        w1_raw = sb([P, PACK, H], F32, "w1_raw")
+        w2_raw = sb([P, PACK, N], F32, "w2_raw")
+        gates = [sb([P, N // P, V], F32, f"gate{d}") for d in range(D)]
+
+        xv = xT.rearrange("(p j) t -> p j t", j=PACK)
+        nc.sync.dma_start(out=x_raw[0][:], in_=xv[:, 0, :])
+        nc.sync.dma_start(offs_sb[:], offs)
+        for j in range(1, 3):
+            nc.sync.dma_start(out=x_raw[j][:], in_=xv[:, j, :])
+        nc.sync.dma_start(out=w1_raw[:], in_=w1.rearrange("(p j) c -> p j c", j=PACK))
+        nc.sync.dma_start(out=x_raw[3][:], in_=xv[:, 3, :])
+        nc.sync.dma_start(out=w2_raw[:], in_=w2.rearrange("(p j) c -> p j c", j=PACK))
+        for d, p in enumerate((pos1, pos2, pos3, pos4)):
+            nc.sync.dma_start(pos_sb[d][:], p)
+            nc.sync.dma_start(out=gates[d][:], in_=gate[d].rearrange("(b p) v -> p b v", p=P))
+
+        x_got = sb([P, 2, S], F32, "x_got")
+        x_group = [sb([P, SLICE, PACK], BF16, f"x_group{s}") for s in range(SLICES)]
+        x_codes = [sb([P, SLICE], U32, f"x_codes{s}") for s in range(SLICES)]
+        x_scales = [sb([P, SLICE], U8, f"x_scales{s}") for s in range(SLICES)]
+        nc.vector.tensor_copy(x_got[:, 0, :], x_raw[0][:].indirect(offs_sb[:]))
+        for s in range(SLICES):
+            cols = slice(s * SLICE // LANE, (s + 1) * SLICE // LANE)
+            nc.vector.tensor_copy(x_got[:, 1, s * SLICE : (s + 1) * SLICE], x_raw[1][:].indirect(offs_sb[:, cols]))
+            nc.scalar.copy(x_group[s][:, :, 0:2], x_got[:, :, s * SLICE : (s + 1) * SLICE].rearrange("p j n -> p n j"))
+
+        def gather_into(s, j):
+            cols = slice(s * SLICE // LANE, (s + 1) * SLICE // LANE)
+            nc.vector.tensor_copy(x_group[s][:, :, j], x_raw[j][:].indirect(offs_sb[:, cols]))
+
+        for s in range(SLICES):
+            gather_into(s, 2)
+
+        w1_group = sb([P, H * PACK], BF16, "w1_group")
+        w1_codes = sb([P, H], U32, "w1_codes")
+        w1_scales = sb([P, H], U8, "w1_scales")
+        w1_out = w1_group[:].rearrange("p (t m j) -> p m j t", t=PACK, j=PACK)
+        w1_in = w1_raw[:].rearrange("p j (m t) -> p m j t", t=PACK)
+        nc.scalar.copy(w1_out[:, 0:64], w1_in[:, 0:64])
+        nc.vector.tensor_copy(w1_out[:, 64:128], w1_in[:, 64:128])
+        nc.vector.quantize_mx(out=w1_codes[:].bitcast(FP8X4), scales=w1_scales[:], in_=w1_group[:])
+
+        y_psum = [psum.tile([P, SLICE], F32, name=f"y_psum{s}") for s in range(SLICES)]
+        for b in range(2):
+            warm = psum.tile([P, H], F32, name="h_bank", bufs=5)
+            nc.tensor.matmul_mx(
+                out=warm[:],
+                lhsT=w1_codes[:, 0:P].bitcast(FP8X4),
+                lhsT_scale=w1_scales[:, 0:P],
+                rhs=w1_codes[:].bitcast(FP8X4),
+                rhs_scale=w1_scales[:],
+                start=True,
+                stop=True,
+            )
+
+        def quantize_x(s):
+            nc.vector.quantize_mx(
+                out=x_codes[s][:].bitcast(FP8X4), scales=x_scales[s][:], in_=x_group[s][:].rearrange("p n j -> p (n j)")
+            )
+
+        w2_group = [sb([P, P, PACK], BF16, f"w2_group{b}") for b in range(2)]
+        w2_codes = [sb([P, P], U32, f"w2_codes{b}") for b in range(2)]
+        w2_scales = [sb([P, P], U8, f"w2_scales{b}") for b in range(2)]
+
+        def interleave_w2(b):
+            nc.scalar.copy(w2_group[b][:], w2_raw[:, :, b * P : (b + 1) * P].rearrange("p j n -> p n j"))
+
+        def quantize_w2(b):
+            nc.vector.quantize_mx(
+                out=w2_codes[b][:].bitcast(FP8X4), scales=w2_scales[b][:], in_=w2_group[b][:].rearrange("p n j -> p (n j)")
+            )
+
+        h_group = [sb([P, SLICE, PACK], BF16, f"h_group{s}") for s in range(SLICES)]
+        h_codes = [sb([P, SLICE], U32, f"h_codes{s}") for s in range(SLICES)]
+        h_scales = [sb([P, SLICE], U8, f"h_scales{s}") for s in range(SLICES)]
+
+        def first(s, half, engine):
+            bank = psum.tile([P, PACK, P], F32, name="h_bank", bufs=5)
+            cols = slice(half * P, (half + 1) * P)
+            for t in range(PACK):
+                nc.tensor.matmul_mx(
+                    out=bank[:, t, :],
+                    lhsT=w1_codes[:, t * P : (t + 1) * P].bitcast(FP8X4),
+                    lhsT_scale=w1_scales[:, t * P : (t + 1) * P],
+                    rhs=x_codes[s][:, cols].bitcast(FP8X4),
+                    rhs_scale=x_scales[s][:, cols],
+                    start=True,
+                    stop=True,
+                )
+            dst, src = h_group[s][:, cols, :], bank[:].rearrange("p t n -> p n t")
+            if engine == "scalar":
+                nc.scalar.activation(dst, src, RELU)
+            else:
+                nc.vector.tensor_scalar_max(dst, src, 0.0)
+
+        def quantize_h(s):
+            nc.vector.quantize_mx(
+                out=h_codes[s][:].bitcast(FP8X4), scales=h_scales[s][:], in_=h_group[s][:].rearrange("p n j -> p (n j)")
+            )
+
+
+        def second(s, b):
+            dst = y_psum[s][:] if b == 0 else y1_psum[s // 2][:, s % 2 * SLICE : (s % 2 + 1) * SLICE]
+            nc.tensor.matmul_mx(
+                out=dst,
+                lhsT=w2_codes[b][:].bitcast(FP8X4),
+                lhsT_scale=w2_scales[b][:],
+                rhs=h_codes[s][:].bitcast(FP8X4),
+                rhs_scale=h_scales[s][:],
+                start=True,
+                stop=True,
+            )
+
+        gather_into(0, 3)
+        gather_into(1, 3)
+        quantize_x(0)
+        interleave_w2(0)
+        first(0, 0, "scalar")
+        first(0, 1, "scalar")
+        gather_into(2, 3)
+        quantize_x(1)
+        first(1, 0, "scalar")
+        quantize_x(2)
+        quantize_w2(0)
+        first(1, 1, "vector")
+        quantize_h(0)
+        first(2, 0, "scalar")
+        interleave_w2(1)
+        first(2, 1, "vector")
+        y = [sb([P, S], F32, f"y{b}") for b in range(2)]
+
+        def leave(engine, s):
+            engine(y[0][:, s * SLICE : (s + 1) * SLICE], y_psum[s][:])
+
+        second(0, 0)
+        leave(nc.scalar.copy, 0)
+        quantize_h(1)
+        second(1, 0)
+        leave(nc.scalar.copy, 1)
+        quantize_h(2)
+        quantize_w2(1)
+        second(2, 0)
+        leave(nc.vector.tensor_copy, 2)
+        turn = [sb([P, D, V], F32, f"turn{b}") for b in range(2)]
+        pair = [sb([P, 2, V], F32, f"pair{b}") for b in range(2)]
+        result = [sb([P, V], F32, f"result{b}") for b in range(2)]
+
+        def fetch(b, d, cols=slice(0, V)):
+            places = pos_sb[d][:, cols.start // LANE : cols.stop // LANE]
+            nc.vector.tensor_tensor(turn[b][:, d, cols], y[b][:].indirect(places), gates[d][:, b, cols], MULT)
+
+        def store(b, cols):
+            nc.sync.dma_start(out=out[b * P : (b + 1) * P, cols], in_=result[b][:, cols])
+
+        fetch(0, 0)
+        y1_psum = [psum.tile([P, 2 * SLICE], F32, name="h_bank", bufs=5) for i in range(2)]
+        for s in range(SLICES):
+            second(s, 1)
+        nc.scalar.copy(y[1][:, 0 : 2 * SLICE], y1_psum[0][:])
+        nc.scalar.copy(y[1][:, 2 * SLICE : S], y1_psum[1][:, 0:SLICE])
+        for d in range(1, D):
+            fetch(0, d)
+        fetch(1, 0)
+        fetch(1, 1)
+        nc.vector.tensor_tensor(pair[0][:], turn[0][:, 0:2, :], turn[0][:, 2:4, :], ADD)
+        nc.vector.tensor_tensor(pair[1][:, 0, :], turn[1][:, 0, :], turn[1][:, 1, :], ADD)
+        fetch(1, 2)
+        nc.vector.tensor_tensor(result[0][:], pair[0][:, 0, :], pair[0][:, 1, :], ADD)
+        store(0, slice(0, V))
+        nc.vector.tensor_tensor(pair[1][:, 1, :], pair[1][:, 0, :], turn[1][:, 2, :], ADD)
+        ends = [slice(0, 256), slice(256, V)]
+        for cols in ends:
+            fetch(1, 3, cols)
+        for cols in ends:
+            nc.vector.tensor_tensor(result[1][:, cols], pair[1][:, 1, cols], turn[1][:, 3, cols], ADD)
+            store(1, cols)

@@ -1,6 +1,7 @@
 from contextlib import ExitStack
 
 import concourse.mybir as mybir
+from concourse.masks import make_identity
 
 K, T, D, S, V, H, N = 512, 2048, 4, 768, 384, 512, 256
 FLOPS = 2 * S * (K * H + H * N)
@@ -49,6 +50,9 @@ def tile_picked_sub_mlp_relu_sub_e_kernel(tc, xT, w1, w2, gate, offs, pos1, pos2
         for d, p in enumerate((pos1, pos2, pos3, pos4)):
             nc.sync.dma_start(pos_sb[d][:], p)
             nc.sync.dma_start(out=gates[d][:], in_=gate[d].rearrange("(b p) v -> p b v", p=P))
+
+        identity = sb([P, P], F32, "identity")
+        make_identity(nc, identity[:])
 
         x_got = sb([P, 2, S], F32, "x_got")
         x_group = [sb([P, SLICE, PACK], BF16, f"x_group{s}") for s in range(SLICES)]
@@ -177,16 +181,20 @@ def tile_picked_sub_mlp_relu_sub_e_kernel(tc, xT, w1, w2, gate, offs, pos1, pos2
         quantize_w2(1)
         second(2, 0)
         leave(nc.vector.tensor_copy, 2)
-        turn = [sb([P, D, V], F32, f"turn{b}") for b in range(2)]
-        pair = [sb([P, 2, V], F32, f"pair{b}") for b in range(2)]
+        turn = [[sb([P, V], F32, f"turn{b}_{d}") for d in range(D)] for b in range(2)]
+        flipped = [sb([P, V], F32, f"flipped{b}") for b in range(2)]
         result = [sb([P, V], F32, f"result{b}") for b in range(2)]
+        pieces = [slice(c * P, (c + 1) * P) for c in range(V // P)]
 
         def fetch(b, d, cols=slice(0, V)):
             places = pos_sb[d][:, cols.start // LANE : cols.stop // LANE]
-            nc.vector.tensor_tensor(turn[b][:, d, cols], y[b][:].indirect(places), gates[d][:, b, cols], MULT)
+            nc.vector.tensor_tensor(turn[b][d][:, cols], y[b][:].indirect(places), gates[d][:, b, cols], MULT)
 
         def store(b, cols):
             nc.sync.dma_start(out=out[b * P : (b + 1) * P, cols], in_=result[b][:, cols])
+
+        def flip(bank, src, start=True, stop=True):
+            nc.tensor.matmul(bank, src, identity[:], start=start, stop=stop, is_transpose=True)
 
         fetch(0, 0)
         y1_psum = [psum.tile([P, 2 * SLICE], F32, name="h_bank", bufs=5) for i in range(2)]
@@ -194,19 +202,34 @@ def tile_picked_sub_mlp_relu_sub_e_kernel(tc, xT, w1, w2, gate, offs, pos1, pos2
             second(s, 1)
         nc.scalar.copy(y[1][:, 0 : 2 * SLICE], y1_psum[0][:])
         nc.scalar.copy(y[1][:, 2 * SLICE : S], y1_psum[1][:, 0:SLICE])
-        for d in range(1, D):
-            fetch(0, d)
-        fetch(1, 0)
-        fetch(1, 1)
-        nc.vector.tensor_tensor(pair[0][:], turn[0][:, 0:2, :], turn[0][:, 2:4, :], ADD)
-        nc.vector.tensor_tensor(pair[1][:, 0, :], turn[1][:, 0, :], turn[1][:, 1, :], ADD)
-        fetch(1, 2)
-        nc.vector.tensor_tensor(result[0][:], pair[0][:, 0, :], pair[0][:, 1, :], ADD)
+
+        sums0 = [psum.tile([P, P], F32, name=f"y_psum{c}") for c in range(len(pieces))]
+        for d in range(D):
+            if d > 0:
+                fetch(0, d)
+            for c, cols in enumerate(pieces):
+                flip(sums0[c][:], turn[0][d][:, cols], d == 0, d == D - 1)
+        back0 = psum.tile([P, V], F32, name="h_bank", bufs=5)
+        for c, cols in enumerate(pieces):
+            nc.scalar.copy(flipped[0][:, cols], sums0[c][:])
+            flip(back0[:, cols], flipped[0][:, cols])
+        nc.scalar.copy(result[0][:], back0[:])
         store(0, slice(0, V))
-        nc.vector.tensor_tensor(pair[1][:, 1, :], pair[1][:, 0, :], turn[1][:, 2, :], ADD)
+
+        sums1 = [psum.tile([P, P], F32, name="h_bank", bufs=5) for c in range(len(pieces))]
+        for d in range(2):
+            fetch(1, d)
+            for c, cols in enumerate(pieces):
+                flip(sums1[c][:], turn[1][d][:, cols], d == 0, False)
+        back1 = [psum.tile([P, 2 * P], F32, name=f"y_psum{i}") for i in range(2)]
+        for c, cols in enumerate(pieces):
+            fetch(1, 2, cols)
+            flip(sums1[c][:], turn[1][2][:, cols], False, True)
+            nc.scalar.copy(flipped[1][:, cols], sums1[c][:])
+            flip(back1[c // 2][:, c % 2 * P : (c % 2 + 1) * P], flipped[1][:, cols])
         ends = [slice(0, 256), slice(256, V)]
         for cols in ends:
             fetch(1, 3, cols)
-        for cols in ends:
-            nc.vector.tensor_tensor(result[1][:, cols], pair[1][:, 1, cols], turn[1][:, 3, cols], ADD)
+        for i, cols in enumerate(ends):
+            nc.vector.tensor_tensor(result[1][:, cols], back1[i][:, 0 : cols.stop - cols.start], turn[1][3][:, cols], ADD)
             store(1, cols)

@@ -14,6 +14,7 @@ U8 = mybir.dt.uint8
 FP8X4 = mybir.dt.float8_e4m3fn_x4
 ADD, MULT = mybir.AluOpType.add, mybir.AluOpType.mult
 RELU = mybir.ActivationFunctionType.Relu
+COPY = mybir.ActivationFunctionType.Copy
 
 P = 128
 PACK = 4
@@ -37,7 +38,7 @@ def tile_picked_sub_mlp_relu_sub_e_kernel(tc, xT, w1, w2, gate, offs, pos1, pos2
         x_raw = [sb([P, T], F32, f"x_raw{j}") for j in range(PACK)]
         w1_raw = sb([P, PACK, H], F32, "w1_raw")
         w2_raw = sb([P, PACK, N], F32, "w2_raw")
-        gates = [sb([P, N // P, V], F32, f"gate{d}") for d in range(D)]
+        gates = sb([P, D, V], F32, "gates")
 
         xv = xT.rearrange("(p j) t -> p j t", j=PACK)
         nc.sync.dma_start(out=x_raw[0][:], in_=xv[:, 0, :])
@@ -45,30 +46,42 @@ def tile_picked_sub_mlp_relu_sub_e_kernel(tc, xT, w1, w2, gate, offs, pos1, pos2
         for j in range(1, 3):
             nc.sync.dma_start(out=x_raw[j][:], in_=xv[:, j, :])
         nc.sync.dma_start(out=w1_raw[:], in_=w1.rearrange("(p j) c -> p j c", j=PACK))
-        nc.sync.dma_start(out=x_raw[3][:], in_=xv[:, 3, :])
+        chunks = [slice(c * T // 4, (c + 1) * T // 4) for c in range(4)]
+        for cols in chunks:
+            nc.sync.dma_start(out=x_raw[3][:, cols], in_=xv[:, 3, cols])
         nc.sync.dma_start(out=w2_raw[:], in_=w2.rearrange("(p j) c -> p j c", j=PACK))
+        nc.sync.dma_start(out=gates[:], in_=gate[:, 0:P, :].rearrange("d p v -> p d v"))
         for d, p in enumerate((pos1, pos2, pos3, pos4)):
             nc.sync.dma_start(pos_sb[d][:], p)
-            nc.sync.dma_start(out=gates[d][:], in_=gate[d].rearrange("(b p) v -> p b v", p=P))
 
         identity = sb([P, P], F32, "identity")
         make_identity(nc, identity[:])
 
         x_got = sb([P, 2, S], F32, "x_got")
-        x_group = [sb([P, SLICE, PACK], BF16, f"x_group{s}") for s in range(SLICES)]
-        x_codes = [sb([P, SLICE], U32, f"x_codes{s}") for s in range(SLICES)]
-        x_scales = [sb([P, SLICE], U8, f"x_scales{s}") for s in range(SLICES)]
+        x_got2 = sb([P, SLICE], F32, "x_got2")
+        x_group = [sb([P, 2, P, PACK], BF16, f"x_group{s}") for s in range(SLICES)]
+        x_tail = x_group[2]
+        x_last = sb([P, T], BF16, "x_last")
+        x_codes = [[sb([P, P], U32, f"x_codes{s}_{h}") for h in range(2)] for s in range(SLICES)]
+        x_scales = [[sb([P, P], U8, f"x_scales{s}_{h}") for h in range(2)] for s in range(SLICES)]
+
+        def entries(s):
+            return offs_sb[:, s * SLICE // LANE : (s + 1) * SLICE // LANE]
+
         nc.vector.tensor_copy(x_got[:, 0, :], x_raw[0][:].indirect(offs_sb[:]))
         for s in range(SLICES):
-            cols = slice(s * SLICE // LANE, (s + 1) * SLICE // LANE)
-            nc.vector.tensor_copy(x_got[:, 1, s * SLICE : (s + 1) * SLICE], x_raw[1][:].indirect(offs_sb[:, cols]))
-            nc.scalar.copy(x_group[s][:, :, 0:2], x_got[:, :, s * SLICE : (s + 1) * SLICE].rearrange("p j n -> p n j"))
+            nc.vector.tensor_copy(x_got[:, 1, s * SLICE : (s + 1) * SLICE], x_raw[1][:].indirect(entries(s)))
+            nc.scalar.copy(
+                x_group[s][:, :, :, 0:2],
+                x_got[:, :, s * SLICE : (s + 1) * SLICE].rearrange("p j (h n) -> p h n j", h=2),
+            )
 
         def gather_into(s, j):
-            cols = slice(s * SLICE // LANE, (s + 1) * SLICE // LANE)
-            nc.vector.tensor_copy(x_group[s][:, :, j], x_raw[j][:].indirect(offs_sb[:, cols]))
+            nc.vector.tensor_copy(x_group[s][:, :, :, j], x_raw[j][:].indirect(entries(s)))
 
-        for s in range(SLICES):
+        nc.vector.tensor_copy(x_got2[:], x_raw[2][:].indirect(entries(2)))
+        nc.scalar.copy(x_tail[:, :, :, 2], x_got2[:].rearrange("p (h n) -> p h n", h=2))
+        for s in range(2):
             gather_into(s, 2)
 
         w1_group = sb([P, H * PACK], BF16, "w1_group")
@@ -76,13 +89,17 @@ def tile_picked_sub_mlp_relu_sub_e_kernel(tc, xT, w1, w2, gate, offs, pos1, pos2
         w1_scales = sb([P, H], U8, "w1_scales")
         w1_out = w1_group[:].rearrange("p (t m j) -> p m j t", t=PACK, j=PACK)
         w1_in = w1_raw[:].rearrange("p j (m t) -> p m j t", t=PACK)
-        nc.scalar.copy(w1_out[:, 0:64], w1_in[:, 0:64])
-        nc.vector.tensor_copy(w1_out[:, 64:128], w1_in[:, 64:128])
+        nc.scalar.copy(w1_out[:, 0:32], w1_in[:, 0:32])
+        nc.vector.tensor_copy(w1_out[:, 32:128], w1_in[:, 32:128])
         nc.vector.quantize_mx(out=w1_codes[:].bitcast(FP8X4), scales=w1_scales[:], in_=w1_group[:])
 
-        y_psum = [psum.tile([P, SLICE], F32, name=f"y_psum{s}") for s in range(SLICES)]
+        for cols in chunks:
+            nc.scalar.copy(x_last[:, cols], x_raw[3][:, cols])
+        nc.scalar.activation(x_tail[:, :, :, 3], x_last[:].indirect(entries(2)), COPY)
+
+        y_psum = [psum.tile([P, SLICE], F32, name=f"y_psum{s}") for s in range(SLICES + 1)]
         for b in range(2):
-            warm = psum.tile([P, H], F32, name="h_bank", bufs=5)
+            warm = psum.tile([P, H], F32, name="h_bank", bufs=4)
             nc.tensor.matmul_mx(
                 out=warm[:],
                 lhsT=w1_codes[:, 0:P].bitcast(FP8X4),
@@ -93,21 +110,25 @@ def tile_picked_sub_mlp_relu_sub_e_kernel(tc, xT, w1, w2, gate, offs, pos1, pos2
                 stop=True,
             )
 
-        def quantize_x(s):
+        def quantize_x(s, h):
             nc.vector.quantize_mx(
-                out=x_codes[s][:].bitcast(FP8X4), scales=x_scales[s][:], in_=x_group[s][:].rearrange("p n j -> p (n j)")
+                out=x_codes[s][h][:].bitcast(FP8X4),
+                scales=x_scales[s][h][:],
+                in_=x_group[s][:, h].rearrange("p n j -> p (n j)"),
             )
 
-        w2_group = [sb([P, P, PACK], BF16, f"w2_group{b}") for b in range(2)]
         w2_codes = [sb([P, P], U32, f"w2_codes{b}") for b in range(2)]
         w2_scales = [sb([P, P], U8, f"w2_scales{b}") for b in range(2)]
 
-        def interleave_w2(b):
-            nc.scalar.copy(w2_group[b][:], w2_raw[:, :, b * P : (b + 1) * P].rearrange("p j n -> p n j"))
+        def interleave_w2(engine, group, b):
+            engine(
+                group.rearrange("p (c i) j -> p c j i", i=4),
+                w2_raw[:, :, b * P : (b + 1) * P].rearrange("p j (c i) -> p c j i", i=4),
+            )
 
-        def quantize_w2(b):
+        def quantize_w2(group, b):
             nc.vector.quantize_mx(
-                out=w2_codes[b][:].bitcast(FP8X4), scales=w2_scales[b][:], in_=w2_group[b][:].rearrange("p n j -> p (n j)")
+                out=w2_codes[b][:].bitcast(FP8X4), scales=w2_scales[b][:], in_=group.rearrange("p n j -> p (n j)")
             )
 
         h_group = [sb([P, SLICE, PACK], BF16, f"h_group{s}") for s in range(SLICES)]
@@ -115,80 +136,88 @@ def tile_picked_sub_mlp_relu_sub_e_kernel(tc, xT, w1, w2, gate, offs, pos1, pos2
         h_scales = [sb([P, SLICE], U8, f"h_scales{s}") for s in range(SLICES)]
 
         def first(s, half, engine):
-            bank = psum.tile([P, PACK, P], F32, name="h_bank", bufs=5)
+            bank = psum.tile([P, PACK, P], F32, name="h_bank", bufs=4)
             cols = slice(half * P, (half + 1) * P)
             for t in range(PACK):
                 nc.tensor.matmul_mx(
                     out=bank[:, t, :],
                     lhsT=w1_codes[:, t * P : (t + 1) * P].bitcast(FP8X4),
                     lhsT_scale=w1_scales[:, t * P : (t + 1) * P],
-                    rhs=x_codes[s][:, cols].bitcast(FP8X4),
-                    rhs_scale=x_scales[s][:, cols],
+                    rhs=x_codes[s][half][:].bitcast(FP8X4),
+                    rhs_scale=x_scales[s][half][:],
                     start=True,
                     stop=True,
                 )
-            dst, src = h_group[s][:, cols, :], bank[:].rearrange("p t n -> p n t")
+            dst = h_group[s][:, cols, :].rearrange("p (c i) t -> p c t i", i=2)
+            src = bank[:].rearrange("p t (c i) -> p c t i", i=2)
             if engine == "scalar":
                 nc.scalar.activation(dst, src, RELU)
             else:
                 nc.vector.tensor_scalar_max(dst, src, 0.0)
 
-        def quantize_h(s):
+        def quantize_h(s, cols=slice(0, SLICE)):
             nc.vector.quantize_mx(
-                out=h_codes[s][:].bitcast(FP8X4), scales=h_scales[s][:], in_=h_group[s][:].rearrange("p n j -> p (n j)")
+                out=h_codes[s][:, cols].bitcast(FP8X4),
+                scales=h_scales[s][:, cols],
+                in_=h_group[s][:, cols, :].rearrange("p n j -> p (n j)"),
             )
 
-
-        def second(s, b):
-            dst = y_psum[s][:] if b == 0 else y1_psum[s // 2][:, s % 2 * SLICE : (s % 2 + 1) * SLICE]
+        def second(dst, b, s, cols=slice(0, SLICE)):
             nc.tensor.matmul_mx(
                 out=dst,
                 lhsT=w2_codes[b][:].bitcast(FP8X4),
                 lhsT_scale=w2_scales[b][:],
-                rhs=h_codes[s][:].bitcast(FP8X4),
-                rhs_scale=h_scales[s][:],
+                rhs=h_codes[s][:, cols].bitcast(FP8X4),
+                rhs_scale=h_scales[s][:, cols],
                 start=True,
                 stop=True,
             )
 
+        y = [sb([P, S], F32, f"y{b}") for b in range(2)]
+        w2_first = sb([P, P, PACK], BF16, "w2_first")
+        halves = [slice(0, P), slice(P, SLICE)]
+
         gather_into(0, 3)
         gather_into(1, 3)
-        quantize_x(0)
-        interleave_w2(0)
-        first(0, 0, "scalar")
+        interleave_w2(nc.scalar.copy, w2_first[:], 0)
+        for s in range(2):
+            quantize_x(s, 0)
+            quantize_x(s, 1)
+        quantize_x(2, 0)
+        quantize_x(2, 1)
+        first(0, 0, "vector")
         first(0, 1, "scalar")
-        gather_into(2, 3)
-        quantize_x(1)
-        first(1, 0, "scalar")
-        quantize_x(2)
-        quantize_w2(0)
-        first(1, 1, "vector")
+        first(1, 0, "vector")
+        first(1, 1, "scalar")
+        quantize_w2(w2_first[:], 0)
         quantize_h(0)
         first(2, 0, "scalar")
-        interleave_w2(1)
         first(2, 1, "vector")
-        y = [sb([P, S], F32, f"y{b}") for b in range(2)]
-
-        def leave(engine, s):
-            engine(y[0][:, s * SLICE : (s + 1) * SLICE], y_psum[s][:])
-
-        second(0, 0)
-        leave(nc.scalar.copy, 0)
+        second(y_psum[0][:], 0, 0)
+        nc.scalar.copy(y[0][:, 0:SLICE], y_psum[0][:])
         quantize_h(1)
-        second(1, 0)
-        leave(nc.scalar.copy, 1)
-        quantize_h(2)
-        quantize_w2(1)
-        second(2, 0)
-        leave(nc.vector.tensor_copy, 2)
-        turn = [[sb([P, V], F32, f"turn{b}_{d}") for d in range(D)] for b in range(2)]
+        second(y_psum[1][:], 0, 1)
+        nc.scalar.copy(y[0][:, SLICE : 2 * SLICE], y_psum[1][:])
+        quantize_h(2, halves[0])
+        second(y_psum[3][:, 0:P], 0, 2, halves[0])
+        quantize_h(2, halves[1])
+        second(y_psum[2][:, 0:P], 0, 2, halves[1])
+        nc.scalar.copy(y[0][:, 2 * SLICE : 2 * SLICE + P], y_psum[3][:, 0:P])
+        nc.vector.tensor_copy(y[0][:, 2 * SLICE + P : S], y_psum[2][:, 0:P])
+        w2_second = h_group[2][:, 0:P, :]
+        interleave_w2(nc.vector.tensor_copy, w2_second, 1)
+        quantize_w2(w2_second, 1)
+
+        turn = [[sb([P, V], F32, f"turn{b}_{d}") for d in range(D - 1)] for b in range(2)]
+        for b in range(2):
+            turn[b].append(turn[1][b])
         flipped = [sb([P, V], F32, f"flipped{b}") for b in range(2)]
         result = [sb([P, V], F32, f"result{b}") for b in range(2)]
         pieces = [slice(c * P, (c + 1) * P) for c in range(V // P)]
 
         def fetch(b, d, cols=slice(0, V)):
             places = pos_sb[d][:, cols.start // LANE : cols.stop // LANE]
-            nc.vector.tensor_tensor(turn[b][d][:, cols], y[b][:].indirect(places), gates[d][:, b, cols], MULT)
+            nc.vector.tensor_tensor(turn[b][d][:, cols], y[b][:].indirect(places), gates[:, d, cols], MULT)
 
         def store(b, cols):
             nc.sync.dma_start(out=out[b * P : (b + 1) * P, cols], in_=result[b][:, cols])
@@ -197,39 +226,38 @@ def tile_picked_sub_mlp_relu_sub_e_kernel(tc, xT, w1, w2, gate, offs, pos1, pos2
             nc.tensor.matmul(bank, src, identity[:], start=start, stop=stop, is_transpose=True)
 
         fetch(0, 0)
-        y1_psum = [psum.tile([P, 2 * SLICE], F32, name="h_bank", bufs=5) for i in range(2)]
+        y1_psum = [psum.tile([P, 2 * SLICE], F32, name="h_bank", bufs=4) for i in range(2)]
         for s in range(SLICES):
-            second(s, 1)
+            second(y1_psum[s // 2][:, s % 2 * SLICE : (s % 2 + 1) * SLICE], 1, s)
         nc.scalar.copy(y[1][:, 0 : 2 * SLICE], y1_psum[0][:])
         nc.scalar.copy(y[1][:, 2 * SLICE : S], y1_psum[1][:, 0:SLICE])
 
-        sums0 = [psum.tile([P, P], F32, name=f"y_psum{c}") for c in range(len(pieces))]
-        for d in range(D):
-            if d > 0:
-                fetch(0, d)
+        def partial_sum(b, sums, backs):
+            for d in range(D - 1):
+                if (b, d) != (0, 0):
+                    fetch(b, d)
+                for c, cols in enumerate(pieces):
+                    flip(sums[c][:], turn[b][d][:, cols], d == 0, d == D - 2)
             for c, cols in enumerate(pieces):
-                flip(sums0[c][:], turn[0][d][:, cols], d == 0, d == D - 1)
-        back0 = psum.tile([P, V], F32, name="h_bank", bufs=5)
-        for c, cols in enumerate(pieces):
-            nc.scalar.copy(flipped[0][:, cols], sums0[c][:])
-            flip(back0[:, cols], flipped[0][:, cols])
-        nc.scalar.copy(result[0][:], back0[:])
-        store(0, slice(0, V))
+                nc.scalar.copy(flipped[b][:, cols], sums[c][:])
+            for c, cols in enumerate(pieces):
+                flip(backs[:, cols], flipped[b][:, cols])
 
-        sums1 = [psum.tile([P, P], F32, name="h_bank", bufs=5) for c in range(len(pieces))]
-        for d in range(2):
-            fetch(1, d)
-            for c, cols in enumerate(pieces):
-                flip(sums1[c][:], turn[1][d][:, cols], d == 0, False)
-        back1 = [psum.tile([P, 2 * P], F32, name=f"y_psum{i}") for i in range(2)]
-        for c, cols in enumerate(pieces):
-            fetch(1, 2, cols)
-            flip(sums1[c][:], turn[1][2][:, cols], False, True)
-            nc.scalar.copy(flipped[1][:, cols], sums1[c][:])
-            flip(back1[c // 2][:, c % 2 * P : (c % 2 + 1) * P], flipped[1][:, cols])
+        sums0 = [psum.tile([P, P], F32, name=f"y_psum{c}") for c in range(len(pieces))]
+        back0 = psum.tile([P, V], F32, name="h_bank", bufs=4)
+        partial_sum(0, sums0, back0)
+        sums1 = [psum.tile([P, P], F32, name=f"y_psum{c}") for c in range(len(pieces))]
+        back1 = psum.tile([P, V], F32, name="h_bank", bufs=4)
+        partial_sum(1, sums1, back1)
+
+        def finish(b, backs, cols):
+            nc.vector.tensor_tensor(result[b][:, cols], backs[:, cols], turn[b][3][:, cols], ADD)
+            store(b, cols)
+
         ends = [slice(0, 256), slice(256, V)]
+        fetch(0, 3)
+        fetch(1, 3, ends[0])
+        finish(0, back0, slice(0, V))
+        fetch(1, 3, ends[1])
         for cols in ends:
-            fetch(1, 3, cols)
-        for i, cols in enumerate(ends):
-            nc.vector.tensor_tensor(result[1][:, cols], back1[i][:, 0 : cols.stop - cols.start], turn[1][3][:, cols], ADD)
-            store(1, cols)
+            finish(1, back1, cols)

@@ -187,12 +187,12 @@ def tile_picked_sub_mlp_relu_sub_e_kernel(tc, xT, w1, w2, gate, offs, pos1, pos2
         quantize_x(2, 1)
         first(0, 0, "vector")
         first(0, 1, "scalar")
-        first(1, 0, "vector")
-        first(1, 1, "scalar")
+        first(1, 0, "scalar")
+        first(1, 1, "vector")
         quantize_w2(w2_first[:], 0)
         quantize_h(0)
         first(2, 0, "scalar")
-        first(2, 1, "vector")
+        first(2, 1, "scalar")
         second(y_psum[0][:], 0, 0)
         nc.scalar.copy(y[0][:, 0:SLICE], y_psum[0][:])
         quantize_h(1)

@@ -36,20 +36,21 @@ def tile_picked_sub_mlp_relu_sub_e_kernel(tc, xT, w1, w2, gate, offs, pos1, pos2
         pos_sb = [keep.tile([P, V // LANE], U16, name=f"pos_sb{d}") for d in range(D)]
 
         x_raw = [sb([P, T], F32, f"x_raw{j}") for j in range(PACK)]
-        w1_raw = sb([P, PACK, H], F32, "w1_raw")
-        w2_raw = sb([P, PACK, N], F32, "w2_raw")
+        w1_raw = [sb([P, PACK, P], F32, f"w1_raw{q}") for q in range(PACK)]
+        w2_raw = [sb([P, PACK, P], F32, f"w2_raw{b}") for b in range(2)]
         gates = sb([P, D, V], F32, "gates")
 
         xv = xT.rearrange("(p j) t -> p j t", j=PACK)
+        w1v = w1.rearrange("(p j) c -> p j c", j=PACK)
+        w2v = w2.rearrange("(p j) c -> p j c", j=PACK)
         nc.sync.dma_start(out=x_raw[0][:], in_=xv[:, 0, :])
         nc.sync.dma_start(offs_sb[:], offs)
-        for j in range(1, 3):
+        for j in (1, 2, 3):
             nc.sync.dma_start(out=x_raw[j][:], in_=xv[:, j, :])
-        nc.sync.dma_start(out=w1_raw[:], in_=w1.rearrange("(p j) c -> p j c", j=PACK))
-        chunks = [slice(c * T // 4, (c + 1) * T // 4) for c in range(4)]
-        for cols in chunks:
-            nc.sync.dma_start(out=x_raw[3][:, cols], in_=xv[:, 3, cols])
-        nc.sync.dma_start(out=w2_raw[:], in_=w2.rearrange("(p j) c -> p j c", j=PACK))
+        for q in range(PACK):
+            nc.sync.dma_start(out=w1_raw[q][:], in_=w1v[:, :, q * P : (q + 1) * P])
+        for b in range(2):
+            nc.sync.dma_start(out=w2_raw[b][:], in_=w2v[:, :, b * P : (b + 1) * P])
         nc.sync.dma_start(out=gates[:], in_=gate[:, 0:P, :].rearrange("d p v -> p d v"))
         for d, p in enumerate((pos1, pos2, pos3, pos4)):
             nc.sync.dma_start(pos_sb[d][:], p)
@@ -58,64 +59,90 @@ def tile_picked_sub_mlp_relu_sub_e_kernel(tc, xT, w1, w2, gate, offs, pos1, pos2
         make_identity(nc, identity[:])
 
         x_got = sb([P, 2, S], F32, "x_got")
-        x_got2 = sb([P, SLICE], F32, "x_got2")
-        x_group = [sb([P, 2, P, PACK], BF16, f"x_group{s}") for s in range(SLICES)]
-        x_tail = x_group[2]
-        x_last = sb([P, T], BF16, "x_last")
-        x_codes = [[sb([P, P], U32, f"x_codes{s}_{h}") for h in range(2)] for s in range(SLICES)]
-        x_scales = [[sb([P, P], U8, f"x_scales{s}_{h}") for h in range(2)] for s in range(SLICES)]
+        x_woven = sb([P, 4, P, PACK], BF16, "x_woven")
+        x_middle = sb([P, 2, P, PACK], BF16, "x_middle")
+        x_group = [x_woven[:, 1:3], x_middle[:], x_woven[:, 0:4:3]]
+        x_scales = [sb([P, SLICE], U8, f"x_scales{s}") for s in range(SLICES)]
 
         def entries(s):
             return offs_sb[:, s * SLICE // LANE : (s + 1) * SLICE // LANE]
 
+        def gather_into(s, j):
+            nc.vector.tensor_copy(x_group[s][:, :, :, j], x_raw[j][:].indirect(entries(s)))
+
         nc.vector.tensor_copy(x_got[:, 0, :], x_raw[0][:].indirect(offs_sb[:]))
-        for s in range(SLICES):
-            nc.vector.tensor_copy(x_got[:, 1, s * SLICE : (s + 1) * SLICE], x_raw[1][:].indirect(entries(s)))
-            nc.scalar.copy(
+
+        def pair(engine, s):
+            engine(
                 x_group[s][:, :, :, 0:2],
                 x_got[:, :, s * SLICE : (s + 1) * SLICE].rearrange("p j (h n) -> p h n j", h=2),
             )
 
-        def gather_into(s, j):
-            nc.vector.tensor_copy(x_group[s][:, :, :, j], x_raw[j][:].indirect(entries(s)))
-
-        nc.vector.tensor_copy(x_got2[:], x_raw[2][:].indirect(entries(2)))
-        nc.scalar.copy(x_tail[:, :, :, 2], x_got2[:].rearrange("p (h n) -> p h n", h=2))
-        for s in range(2):
+        for s in (2, 0, 1):
+            nc.vector.tensor_copy(x_got[:, 1, s * SLICE : (s + 1) * SLICE], x_raw[1][:].indirect(entries(s)))
+        pair(nc.scalar.copy, 2)
+        pair(nc.vector.tensor_copy, 0)
+        pair(nc.scalar.copy, 1)
+        for s in (2, 0, 1):
             gather_into(s, 2)
+        for s in range(2):
+            gather_into(s, 3)
 
-        w1_group = sb([P, H * PACK], BF16, "w1_group")
+        w1_half = [sb([P, PACK, P // 2, PACK], BF16, f"w1_half{h}") for h in range(2)]
         w1_codes = sb([P, H], U32, "w1_codes")
         w1_scales = sb([P, H], U8, "w1_scales")
-        w1_out = w1_group[:].rearrange("p (t m j) -> p m j t", t=PACK, j=PACK)
-        w1_in = w1_raw[:].rearrange("p j (m t) -> p m j t", t=PACK)
-        nc.scalar.copy(w1_out[:, 0:32], w1_in[:, 0:32])
-        nc.vector.tensor_copy(w1_out[:, 32:128], w1_in[:, 32:128])
-        nc.vector.quantize_mx(out=w1_codes[:].bitcast(FP8X4), scales=w1_scales[:], in_=w1_group[:])
+        for q in range(PACK):
+            nc.scalar.copy(
+                w1_half[q // 2][:, :, q % 2 * 32 : (q % 2 + 1) * 32, :].rearrange("p t m j -> p m j t"),
+                w1_raw[q][:].rearrange("p j (m t) -> p m j t", t=PACK),
+            )
 
-        for cols in chunks:
-            nc.scalar.copy(x_last[:, cols], x_raw[3][:, cols])
-        nc.scalar.activation(x_tail[:, :, :, 3], x_last[:].indirect(entries(2)), COPY)
+        def quantize_w1(h):
+            for t in range(PACK):
+                cols = slice(t * P + h * P // 2, t * P + (h + 1) * P // 2)
+                nc.vector.quantize_mx(
+                    out=w1_codes[:, cols].bitcast(FP8X4),
+                    scales=w1_scales[:, cols],
+                    in_=w1_half[h][:, t].rearrange("p m j -> p (m j)"),
+                )
 
+        x_codes = []
+
+        def quantize_x(s, name):
+            x_codes.append(sb([P, SLICE], U32, name))
+            if s < 2:
+                nc.vector.quantize_mx(
+                    out=x_codes[s][:].bitcast(FP8X4),
+                    scales=x_scales[s][:],
+                    in_=x_group[s].rearrange("p h n j -> p (h n j)"),
+                )
+            else:
+                for h in range(2):
+                    nc.vector.quantize_mx(
+                        out=x_codes[s][:, h * P : (h + 1) * P].bitcast(FP8X4),
+                        scales=x_scales[s][:, h * P : (h + 1) * P],
+                        in_=x_group[s][:, h].rearrange("p n j -> p (n j)"),
+                    )
+
+        quantize_x(0, "x_codes0")
         y_psum = [psum.tile([P, SLICE], F32, name=f"y_psum{s}") for s in range(SLICES + 1)]
         for b in range(2):
-            warm = psum.tile([P, H], F32, name="h_bank", bufs=4)
-            nc.tensor.matmul_mx(
-                out=warm[:],
-                lhsT=w1_codes[:, 0:P].bitcast(FP8X4),
-                lhsT_scale=w1_scales[:, 0:P],
-                rhs=w1_codes[:].bitcast(FP8X4),
-                rhs_scale=w1_scales[:],
-                start=True,
-                stop=True,
-            )
-
-        def quantize_x(s, h):
-            nc.vector.quantize_mx(
-                out=x_codes[s][h][:].bitcast(FP8X4),
-                scales=x_scales[s][h][:],
-                in_=x_group[s][:, h].rearrange("p n j -> p (n j)"),
-            )
+            warm = psum.tile([P, 2, SLICE], F32, name="h_bank", bufs=4)
+            for i in range(2):
+                nc.tensor.matmul_mx(
+                    out=warm[:, i, :],
+                    lhsT=x_codes[0][:, 0:P].bitcast(FP8X4),
+                    lhsT_scale=x_scales[0][:, 0:P],
+                    rhs=x_codes[0][:].bitcast(FP8X4),
+                    rhs_scale=x_scales[0][:],
+                    start=True,
+                    stop=True,
+                )
+        quantize_x(1, "x_codes1")
+        gather_into(2, 3)
+        quantize_w1(0)
+        quantize_w1(1)
+        quantize_x(2, "w1_half1")
 
         w2_codes = [sb([P, P], U32, f"w2_codes{b}") for b in range(2)]
         w2_scales = [sb([P, P], U8, f"w2_scales{b}") for b in range(2)]
@@ -123,7 +150,7 @@ def tile_picked_sub_mlp_relu_sub_e_kernel(tc, xT, w1, w2, gate, offs, pos1, pos2
         def interleave_w2(engine, group, b):
             engine(
                 group.rearrange("p (c i) j -> p c j i", i=4),
-                w2_raw[:, :, b * P : (b + 1) * P].rearrange("p j (c i) -> p c j i", i=4),
+                w2_raw[b][:].rearrange("p j (c i) -> p c j i", i=4),
             )
 
         def quantize_w2(group, b):
@@ -143,8 +170,8 @@ def tile_picked_sub_mlp_relu_sub_e_kernel(tc, xT, w1, w2, gate, offs, pos1, pos2
                     out=bank[:, t, :],
                     lhsT=w1_codes[:, t * P : (t + 1) * P].bitcast(FP8X4),
                     lhsT_scale=w1_scales[:, t * P : (t + 1) * P],
-                    rhs=x_codes[s][half][:].bitcast(FP8X4),
-                    rhs_scale=x_scales[s][half][:],
+                    rhs=x_codes[s][:, cols].bitcast(FP8X4),
+                    rhs_scale=x_scales[s][:, cols],
                     start=True,
                     stop=True,
                 )
@@ -177,19 +204,12 @@ def tile_picked_sub_mlp_relu_sub_e_kernel(tc, xT, w1, w2, gate, offs, pos1, pos2
         w2_first = sb([P, P, PACK], BF16, "w2_first")
         halves = [slice(0, P), slice(P, SLICE)]
 
-        gather_into(0, 3)
-        gather_into(1, 3)
         interleave_w2(nc.scalar.copy, w2_first[:], 0)
-        for s in range(2):
-            quantize_x(s, 0)
-            quantize_x(s, 1)
-        quantize_x(2, 0)
-        quantize_x(2, 1)
-        first(0, 0, "vector")
-        first(0, 1, "scalar")
+        first(0, 0, "scalar")
+        quantize_w2(w2_first[:], 0)
+        first(0, 1, "vector")
         first(1, 0, "scalar")
         first(1, 1, "vector")
-        quantize_w2(w2_first[:], 0)
         quantize_h(0)
         first(2, 0, "scalar")
         first(2, 1, "scalar")

@@ -43,9 +43,9 @@ def tile_picked_sub_mlp_relu_sub_e_kernel(tc, xT, w1, w2, gate, offs, pos1, pos2
         xv = xT.rearrange("(p j) t -> p j t", j=PACK)
         w1v = w1.rearrange("(p j) c -> p j c", j=PACK)
         w2v = w2.rearrange("(p j) c -> p j c", j=PACK)
-        nc.sync.dma_start(out=x_raw[0][:], in_=xv[:, 0, :])
+        nc.sync.dma_start(out=x_raw[2][:], in_=xv[:, 2, :])
         nc.sync.dma_start(offs_sb[:], offs)
-        for j in (1, 2, 3):
+        for j in (0, 1, 3):
             nc.sync.dma_start(out=x_raw[j][:], in_=xv[:, j, :])
         for q in range(PACK):
             nc.sync.dma_start(out=w1_raw[q][:], in_=w1v[:, :, q * P : (q + 1) * P])
@@ -70,6 +70,8 @@ def tile_picked_sub_mlp_relu_sub_e_kernel(tc, xT, w1, w2, gate, offs, pos1, pos2
         def gather_into(s, j):
             nc.vector.tensor_copy(x_group[s][:, :, :, j], x_raw[j][:].indirect(entries(s)))
 
+        for s in range(SLICES):
+            gather_into(s, 2)
         nc.vector.tensor_copy(x_got[:, 0, :], x_raw[0][:].indirect(offs_sb[:]))
 
         def pair(engine, s):
@@ -81,10 +83,8 @@ def tile_picked_sub_mlp_relu_sub_e_kernel(tc, xT, w1, w2, gate, offs, pos1, pos2
         for s in (2, 0, 1):
             nc.vector.tensor_copy(x_got[:, 1, s * SLICE : (s + 1) * SLICE], x_raw[1][:].indirect(entries(s)))
         pair(nc.scalar.copy, 2)
-        pair(nc.vector.tensor_copy, 0)
-        pair(nc.scalar.copy, 1)
-        for s in (2, 0, 1):
-            gather_into(s, 2)
+        pair(nc.scalar.copy, 0)
+        pair(nc.vector.tensor_copy, 1)
         for s in range(2):
             gather_into(s, 3)
 

@@ -58,7 +58,7 @@ def tile_picked_sub_mlp_relu_sub_e_kernel(tc, xT, w1, w2, gate, offs, pos1, pos2
         identity = sb([P, P], F32, "identity")
         make_identity(nc, identity[:])
 
-        x_got = sb([P, 2, S], F32, "x_got")
+        x_got = sb([P, 2, S - SLICE], F32, "x_got")
         x_woven = sb([P, 4, P, PACK], BF16, "x_woven")
         x_middle = sb([P, 2, P, PACK], BF16, "x_middle")
         x_group = [x_woven[:, 1:3], x_middle[:], x_woven[:, 0:4:3]]
@@ -72,19 +72,19 @@ def tile_picked_sub_mlp_relu_sub_e_kernel(tc, xT, w1, w2, gate, offs, pos1, pos2
 
         for s in range(SLICES):
             gather_into(s, 2)
-        nc.vector.tensor_copy(x_got[:, 0, :], x_raw[0][:].indirect(offs_sb[:]))
-
-        def pair(engine, s):
-            engine(
-                x_group[s][:, :, :, 0:2],
-                x_got[:, :, s * SLICE : (s + 1) * SLICE].rearrange("p j (h n) -> p h n j", h=2),
+        nc.vector.tensor_copy(x_got[:, 0, :], x_raw[0][:].indirect(offs_sb[:, SLICE // LANE :]))
+        gather_into(0, 0)
+        for s in (1, 2):
+            nc.vector.tensor_copy(x_got[:, 1, (s - 1) * SLICE : s * SLICE], x_raw[1][:].indirect(entries(s)))
+        gather_into(0, 1)
+        nc.scalar.copy(
+            x_group[1][:, :, :, 0:2], x_got[:, :, 0:SLICE].rearrange("p j (h n) -> p h n j", h=2)
+        )
+        for h in range(2):
+            nc.scalar.copy(
+                x_group[2][:, h, :, 0:2],
+                x_got[:, :, SLICE + h * P : SLICE + (h + 1) * P].rearrange("p j n -> p n j"),
             )
-
-        for s in (2, 0, 1):
-            nc.vector.tensor_copy(x_got[:, 1, s * SLICE : (s + 1) * SLICE], x_raw[1][:].indirect(entries(s)))
-        pair(nc.scalar.copy, 2)
-        pair(nc.scalar.copy, 0)
-        pair(nc.vector.tensor_copy, 1)
         for s in range(2):
             gather_into(s, 3)
 

@@ -138,11 +138,20 @@ def tile_picked_sub_mlp_relu_sub_e_kernel(tc, xT, w1, w2, gate, offs, pos1, pos2
                     start=True,
                     stop=True,
                 )
+        nc.tensor.matmul_mx(
+            out=y_psum[3][:, 0:P],
+            lhsT=x_codes[0][:, 0:P].bitcast(FP8X4),
+            lhsT_scale=x_scales[0][:, 0:P],
+            rhs=x_codes[0][:, 0:P].bitcast(FP8X4),
+            rhs_scale=x_scales[0][:, 0:P],
+            start=True,
+            stop=True,
+        )
         quantize_x(1, "x_codes1")
         gather_into(2, 3)
         quantize_w1(0)
         quantize_w1(1)
-        quantize_x(2, "w1_half1")
+        quantize_x(2, "w1_raw3")
 
         w2_codes = [sb([P, P], U32, f"w2_codes{b}") for b in range(2)]
         w2_scales = [sb([P, P], U8, f"w2_scales{b}") for b in range(2)]
@@ -162,7 +171,7 @@ def tile_picked_sub_mlp_relu_sub_e_kernel(tc, xT, w1, w2, gate, offs, pos1, pos2
         h_codes = [sb([P, SLICE], U32, f"h_codes{s}") for s in range(SLICES)]
         h_scales = [sb([P, SLICE], U8, f"h_scales{s}") for s in range(SLICES)]
 
-        def first(s, half, engine):
+        def first(s, half, engine, parts=1):
             bank = psum.tile([P, PACK, P], F32, name="h_bank", bufs=4)
             cols = slice(half * P, (half + 1) * P)
             for t in range(PACK):
@@ -177,10 +186,12 @@ def tile_picked_sub_mlp_relu_sub_e_kernel(tc, xT, w1, w2, gate, offs, pos1, pos2
                 )
             dst = h_group[s][:, cols, :].rearrange("p (c i) t -> p c t i", i=2)
             src = bank[:].rearrange("p t (c i) -> p c t i", i=2)
-            if engine == "scalar":
-                nc.scalar.activation(dst, src, RELU)
-            else:
-                nc.vector.tensor_scalar_max(dst, src, 0.0)
+            for k in range(parts):
+                pairs = slice(k * P // 2 // parts, (k + 1) * P // 2 // parts)
+                if engine == "scalar":
+                    nc.scalar.activation(dst[:, pairs], src[:, pairs], RELU)
+                else:
+                    nc.vector.tensor_scalar_max(dst[:, pairs], src[:, pairs], 0.0)
 
         def quantize_h(s, cols=slice(0, SLICE)):
             nc.vector.quantize_mx(
@@ -212,18 +223,21 @@ def tile_picked_sub_mlp_relu_sub_e_kernel(tc, xT, w1, w2, gate, offs, pos1, pos2
         first(1, 1, "vector")
         quantize_h(0)
         first(2, 0, "scalar")
-        first(2, 1, "scalar")
+        first(2, 1, "scalar", 2)
         second(y_psum[0][:], 0, 0)
-        nc.scalar.copy(y[0][:, 0:SLICE], y_psum[0][:])
         quantize_h(1)
         second(y_psum[1][:], 0, 1)
         nc.scalar.copy(y[0][:, SLICE : 2 * SLICE], y_psum[1][:])
         quantize_h(2, halves[0])
         second(y_psum[3][:, 0:P], 0, 2, halves[0])
-        quantize_h(2, halves[1])
-        second(y_psum[2][:, 0:P], 0, 2, halves[1])
         nc.scalar.copy(y[0][:, 2 * SLICE : 2 * SLICE + P], y_psum[3][:, 0:P])
-        nc.vector.tensor_copy(y[0][:, 2 * SLICE + P : S], y_psum[2][:, 0:P])
+        nc.vector.tensor_copy(y[0][:, 0:SLICE], y_psum[0][:])
+        last_bank = psum.tile([P, P // 2], F32, name="h_bank", bufs=4)
+        for k, bank in enumerate((y_psum[2][:, 0 : P // 2], last_bank[:])):
+            cols = slice(P + k * P // 2, P + (k + 1) * P // 2)
+            quantize_h(2, cols)
+            second(bank, 0, 2, cols)
+            nc.scalar.copy(y[0][:, 2 * SLICE + cols.start : 2 * SLICE + cols.stop], bank)
         w2_second = h_group[2][:, 0:P, :]
         interleave_w2(nc.vector.tensor_copy, w2_second, 1)
         quantize_w2(w2_second, 1)

@@ -58,10 +58,10 @@ def tile_picked_sub_mlp_relu_sub_e_kernel(tc, xT, w1, w2, gate, offs, pos1, pos2
         identity = sb([P, P], F32, "identity")
         make_identity(nc, identity[:])
 
-        x_got = sb([P, 2, S - SLICE], F32, "x_got")
-        x_woven = sb([P, 4, P, PACK], BF16, "x_woven")
+        x_got = sb([P, 2, SLICE], F32, "x_got")
+        x_woven = sb([P, 2, 6, SLICE], BF16, "x_woven")
         x_middle = sb([P, 2, P, PACK], BF16, "x_middle")
-        x_group = [x_woven[:, 1:3], x_middle[:], x_woven[:, 0:4:3]]
+        x_group = [x_woven[:, 0, 2:6].rearrange("p (h g) (n j) -> p h (g n) j", h=2, j=PACK), x_middle[:]]
         x_scales = [sb([P, SLICE], U8, f"x_scales{s}") for s in range(SLICES)]
 
         def entries(s):
@@ -70,21 +70,18 @@ def tile_picked_sub_mlp_relu_sub_e_kernel(tc, xT, w1, w2, gate, offs, pos1, pos2
         def gather_into(s, j):
             nc.vector.tensor_copy(x_group[s][:, :, :, j], x_raw[j][:].indirect(entries(s)))
 
-        for s in range(SLICES):
+        def gather_pair(j):
+            pairs = x_woven[:, :, j // 2].rearrange("p h (n e) -> p h n e", e=2)
+            nc.vector.tensor_copy(pairs[:, :, :, j % 2], x_raw[j][:].indirect(entries(2)))
+
+        for s in range(2):
             gather_into(s, 2)
-        nc.vector.tensor_copy(x_got[:, 0, :], x_raw[0][:].indirect(offs_sb[:, SLICE // LANE :]))
-        gather_into(0, 0)
-        for s in (1, 2):
-            nc.vector.tensor_copy(x_got[:, 1, (s - 1) * SLICE : s * SLICE], x_raw[1][:].indirect(entries(s)))
-        gather_into(0, 1)
-        nc.scalar.copy(
-            x_group[1][:, :, :, 0:2], x_got[:, :, 0:SLICE].rearrange("p j (h n) -> p h n j", h=2)
-        )
-        for h in range(2):
-            nc.scalar.copy(
-                x_group[2][:, h, :, 0:2],
-                x_got[:, :, SLICE + h * P : SLICE + (h + 1) * P].rearrange("p j n -> p n j"),
-            )
+        gather_pair(2)
+        for j in range(2):
+            gather_into(0, j)
+            nc.vector.tensor_copy(x_got[:, j], x_raw[j][:].indirect(entries(1)))
+            gather_pair(j)
+        nc.scalar.copy(x_group[1][:, :, :, 0:2], x_got[:].rearrange("p j (h n) -> p h n j", h=2))
         for s in range(2):
             gather_into(s, 3)
 
@@ -110,19 +107,11 @@ def tile_picked_sub_mlp_relu_sub_e_kernel(tc, xT, w1, w2, gate, offs, pos1, pos2
 
         def quantize_x(s, name):
             x_codes.append(sb([P, SLICE], U32, name))
-            if s < 2:
-                nc.vector.quantize_mx(
-                    out=x_codes[s][:].bitcast(FP8X4),
-                    scales=x_scales[s][:],
-                    in_=x_group[s].rearrange("p h n j -> p (h n j)"),
-                )
-            else:
-                for h in range(2):
-                    nc.vector.quantize_mx(
-                        out=x_codes[s][:, h * P : (h + 1) * P].bitcast(FP8X4),
-                        scales=x_scales[s][:, h * P : (h + 1) * P],
-                        in_=x_group[s][:, h].rearrange("p n j -> p (n j)"),
-                    )
+            nc.vector.quantize_mx(
+                out=x_codes[s][:].bitcast(FP8X4),
+                scales=x_scales[s][:],
+                in_=x_group[s].rearrange("p h n j -> p (h n j)"),
+            )
 
         quantize_x(0, "x_codes0")
         y_psum = [psum.tile([P, SLICE], F32, name=f"y_psum{s}") for s in range(SLICES + 1)]
@@ -148,10 +137,16 @@ def tile_picked_sub_mlp_relu_sub_e_kernel(tc, xT, w1, w2, gate, offs, pos1, pos2
             stop=True,
         )
         quantize_x(1, "x_codes1")
-        gather_into(2, 3)
+        gather_pair(3)
+        x_quads = sb([P, 2, P, 2], U32, "w1_raw2")
+        nc.scalar.copy(
+            x_quads[:].rearrange("p h (c i) u -> p h c u i", i=2),
+            x_woven[:, :, 0:2].bitcast(U32).rearrange("p h u (c i) -> p h c u i", i=2),
+        )
+        x_group.append(x_quads[:].bitcast(BF16))
         quantize_w1(0)
         quantize_w1(1)
-        quantize_x(2, "w1_raw3")
+        quantize_x(2, "x_codes2")
 
         w2_codes = [sb([P, P], U32, f"w2_codes{b}") for b in range(2)]
         w2_scales = [sb([P, P], U8, f"w2_scales{b}") for b in range(2)]
@@ -212,15 +207,15 @@ def tile_picked_sub_mlp_relu_sub_e_kernel(tc, xT, w1, w2, gate, offs, pos1, pos2
             )
 
         y = [sb([P, S], F32, f"y{b}") for b in range(2)]
-        w2_first = sb([P, P, PACK], BF16, "w2_first")
+        w2_first = sb([P, P, PACK], BF16, "w1_raw2")
         halves = [slice(0, P), slice(P, SLICE)]
 
-        interleave_w2(nc.scalar.copy, w2_first[:], 0)
+        nc.gpsimd.tensor_scalar(w2_first[:], w2_raw[0][:].rearrange("p j n -> p n j"), 1.0, 0.0, MULT, ADD)
         first(0, 0, "scalar")
-        quantize_w2(w2_first[:], 0)
         first(0, 1, "vector")
         first(1, 0, "scalar")
         first(1, 1, "vector")
+        quantize_w2(w2_first[:], 0)
         quantize_h(0)
         first(2, 0, "scalar")
         first(2, 1, "scalar", 2)

@@ -85,22 +85,25 @@ def tile_picked_sub_mlp_relu_sub_e_kernel(tc, xT, w1, w2, gate, offs, pos1, pos2
         for s in range(2):
             gather_into(s, 3)
 
-        w1_half = [sb([P, PACK, P // 2, PACK], BF16, f"w1_half{h}") for h in range(2)]
+        w1_parts = [(0, 64), (64, 96), (96, 128)]
+        w1_part = [sb([P, PACK, b - a, PACK], BF16, f"w1_part{a}") for a, b in w1_parts]
         w1_codes = sb([P, H], U32, "w1_codes")
         w1_scales = sb([P, H], U8, "w1_scales")
-        for q in range(PACK):
-            nc.scalar.copy(
-                w1_half[q // 2][:, :, q % 2 * 32 : (q % 2 + 1) * 32, :].rearrange("p t m j -> p m j t"),
-                w1_raw[q][:].rearrange("p j (m t) -> p m j t", t=PACK),
-            )
+
+        def interleave_w1(engine, dst, src):
+            engine(dst.rearrange("p t m j -> p m j t"), src.rearrange("p j (m t) -> p m j t", t=PACK))
+
+        for q, dst in enumerate((w1_part[0][:, :, 0:32], w1_part[0][:, :, 32:64], w1_part[1][:])):
+            interleave_w1(nc.scalar.copy, dst, w1_raw[q][:])
+        interleave_w1(nc.scalar.copy, w1_part[2][:, :, 0:16], w1_raw[3][:, :, 0:64])
 
         def quantize_w1(h):
             for t in range(PACK):
-                cols = slice(t * P + h * P // 2, t * P + (h + 1) * P // 2)
+                cols = slice(t * P + w1_parts[h][0], t * P + w1_parts[h][1])
                 nc.vector.quantize_mx(
                     out=w1_codes[:, cols].bitcast(FP8X4),
                     scales=w1_scales[:, cols],
-                    in_=w1_half[h][:, t].rearrange("p m j -> p (m j)"),
+                    in_=w1_part[h][:, t].rearrange("p m j -> p (m j)"),
                 )
 
         x_codes = []
@@ -145,7 +148,9 @@ def tile_picked_sub_mlp_relu_sub_e_kernel(tc, xT, w1, w2, gate, offs, pos1, pos2
         )
         x_group.append(x_quads[:].bitcast(BF16))
         quantize_w1(0)
+        interleave_w1(nc.vector.tensor_copy, w1_part[2][:, :, 16:32], w1_raw[3][:, :, 64:128])
         quantize_w1(1)
+        quantize_w1(2)
         quantize_x(2, "x_codes2")
 
         w2_codes = [sb([P, P], U32, f"w2_codes{b}") for b in range(2)]

@@ -59,9 +59,9 @@ def tile_picked_sub_mlp_relu_sub_e_kernel(tc, xT, w1, w2, gate, offs, pos1, pos2
         make_identity(nc, identity[:])
 
         x_got = sb([P, 2, SLICE], F32, "x_got")
-        x_woven = sb([P, 2, 6, SLICE], BF16, "x_woven")
+        x_woven = sb([P, 2, 4, SLICE], BF16, "x_woven")
         x_middle = sb([P, 2, P, PACK], BF16, "x_middle")
-        x_group = [x_woven[:, 0, 2:6].rearrange("p (h g) (n j) -> p h (g n) j", h=2, j=PACK), x_middle[:]]
+        x_group = [x_woven[:, :, 2:4].rearrange("p h g (n j) -> p h (g n) j", j=PACK), x_middle[:]]
         x_scales = [sb([P, SLICE], U8, f"x_scales{s}") for s in range(SLICES)]
 
         def entries(s):
@@ -110,11 +110,14 @@ def tile_picked_sub_mlp_relu_sub_e_kernel(tc, xT, w1, w2, gate, offs, pos1, pos2
 
         def quantize_x(s, name):
             x_codes.append(sb([P, SLICE], U32, name))
-            nc.vector.quantize_mx(
-                out=x_codes[s][:].bitcast(FP8X4),
-                scales=x_scales[s][:],
-                in_=x_group[s].rearrange("p h n j -> p (h n j)"),
-            )
+            parts = 2 if s == 0 else 1
+            for h in range(parts):
+                cols = slice(h * SLICE // parts, (h + 1) * SLICE // parts)
+                nc.vector.quantize_mx(
+                    out=x_codes[s][:, cols].bitcast(FP8X4),
+                    scales=x_scales[s][:, cols],
+                    in_=x_group[s][:, h * 2 // parts : (h + 1) * 2 // parts].rearrange("p h n j -> p (h n j)"),
+                )
 
         quantize_x(0, "x_codes0")
         y_psum = [psum.tile([P, SLICE], F32, name=f"y_psum{s}") for s in range(SLICES + 1)]
@@ -139,7 +142,6 @@ def tile_picked_sub_mlp_relu_sub_e_kernel(tc, xT, w1, w2, gate, offs, pos1, pos2
             start=True,
             stop=True,
         )
-        quantize_x(1, "x_codes1")
         gather_pair(3)
         x_quads = sb([P, 2, P, 2], U32, "w1_raw2")
         nc.scalar.copy(
@@ -151,6 +153,7 @@ def tile_picked_sub_mlp_relu_sub_e_kernel(tc, xT, w1, w2, gate, offs, pos1, pos2
         interleave_w1(nc.vector.tensor_copy, w1_part[2][:, :, 16:32], w1_raw[3][:, :, 64:128])
         quantize_w1(1)
         quantize_w1(2)
+        quantize_x(1, "w1_raw3")
         quantize_x(2, "x_codes2")
 
         w2_codes = [sb([P, P], U32, f"w2_codes{b}") for b in range(2)]

@@ -59,9 +59,9 @@ def tile_picked_sub_mlp_relu_sub_e_kernel(tc, xT, w1, w2, gate, offs, pos1, pos2
         make_identity(nc, identity[:])
 
         x_got = sb([P, 2, SLICE], F32, "x_got")
-        x_woven = sb([P, 2, 4, SLICE], BF16, "x_woven")
-        x_middle = sb([P, 2, P, PACK], BF16, "x_middle")
-        x_group = [x_woven[:, :, 2:4].rearrange("p h g (n j) -> p h (g n) j", j=PACK), x_middle[:]]
+        x_woven = sb([P, 2, 2, P, PACK], BF16, "x_woven")
+        x_pairs = sb([P, 2, SLICE, 2], BF16, "x_pairs")
+        x_group = [x_woven[:, :, 1], x_woven[:, :, 0]]
         x_scales = [sb([P, SLICE], U8, f"x_scales{s}") for s in range(SLICES)]
 
         def entries(s):
@@ -71,19 +71,22 @@ def tile_picked_sub_mlp_relu_sub_e_kernel(tc, xT, w1, w2, gate, offs, pos1, pos2
             nc.vector.tensor_copy(x_group[s][:, :, :, j], x_raw[j][:].indirect(entries(s)))
 
         def gather_pair(j):
-            pairs = x_woven[:, :, j // 2].rearrange("p h (n e) -> p h n e", e=2)
-            nc.vector.tensor_copy(pairs[:, :, :, j % 2], x_raw[j][:].indirect(entries(2)))
+            nc.vector.tensor_copy(x_pairs[:, j // 2, :, j % 2], x_raw[j][:].indirect(entries(2)))
 
         for s in range(2):
             gather_into(s, 2)
         gather_pair(2)
         for j in range(2):
-            gather_into(0, j)
-            nc.vector.tensor_copy(x_got[:, j], x_raw[j][:].indirect(entries(1)))
+            nc.vector.tensor_copy(x_got[:, j], x_raw[j][:].indirect(entries(0)))
+            if j == 1:
+                for h in range(2):
+                    nc.scalar.copy(
+                        x_group[0][:, h, :, 0:2], x_got[:, :, h * P : (h + 1) * P].rearrange("p j n -> p n j")
+                    )
             gather_pair(j)
-        nc.scalar.copy(x_group[1][:, :, :, 0:2], x_got[:].rearrange("p j (h n) -> p h n j", h=2))
-        for s in range(2):
-            gather_into(s, 3)
+            gather_into(1, j)
+        gather_into(0, 3)
+        gather_pair(3)
 
         w1_parts = [(0, 64), (64, 96), (96, 128)]
         w1_part = [sb([P, PACK, b - a, PACK], BF16, f"w1_part{a}") for a, b in w1_parts]
@@ -110,7 +113,7 @@ def tile_picked_sub_mlp_relu_sub_e_kernel(tc, xT, w1, w2, gate, offs, pos1, pos2
 
         def quantize_x(s, name):
             x_codes.append(sb([P, SLICE], U32, name))
-            parts = 2 if s == 0 else 1
+            parts = 2 if s < 2 else 1
             for h in range(parts):
                 cols = slice(h * SLICE // parts, (h + 1) * SLICE // parts)
                 nc.vector.quantize_mx(
@@ -121,6 +124,15 @@ def tile_picked_sub_mlp_relu_sub_e_kernel(tc, xT, w1, w2, gate, offs, pos1, pos2
 
         quantize_x(0, "x_codes0")
         y_psum = [psum.tile([P, SLICE], F32, name=f"y_psum{s}") for s in range(SLICES + 1)]
+        nc.tensor.matmul_mx(
+            out=y_psum[3][:, 0:P],
+            lhsT=x_codes[0][:, 0:P].bitcast(FP8X4),
+            lhsT_scale=x_scales[0][:, 0:P],
+            rhs=x_codes[0][:, 0:P].bitcast(FP8X4),
+            rhs_scale=x_scales[0][:, 0:P],
+            start=True,
+            stop=True,
+        )
         for b in range(2):
             warm = psum.tile([P, 2, SLICE], F32, name="h_bank", bufs=4)
             for i in range(2):
@@ -133,20 +145,11 @@ def tile_picked_sub_mlp_relu_sub_e_kernel(tc, xT, w1, w2, gate, offs, pos1, pos2
                     start=True,
                     stop=True,
                 )
-        nc.tensor.matmul_mx(
-            out=y_psum[3][:, 0:P],
-            lhsT=x_codes[0][:, 0:P].bitcast(FP8X4),
-            lhsT_scale=x_scales[0][:, 0:P],
-            rhs=x_codes[0][:, 0:P].bitcast(FP8X4),
-            rhs_scale=x_scales[0][:, 0:P],
-            start=True,
-            stop=True,
-        )
-        gather_pair(3)
+        gather_into(1, 3)
         x_quads = sb([P, 2, P, 2], U32, "w1_raw2")
         nc.scalar.copy(
             x_quads[:].rearrange("p h (c i) u -> p h c u i", i=2),
-            x_woven[:, :, 0:2].bitcast(U32).rearrange("p h u (c i) -> p h c u i", i=2),
+            x_pairs[:].rearrange("p u n e -> p u (n e)").bitcast(U32).rearrange("p u (h c i) -> p h c u i", h=2, i=2),
         )
         x_group.append(x_quads[:].bitcast(BF16))
         quantize_w1(0)

@@ -47,7 +47,7 @@ def tile_picked_sub_mlp_relu_sub_e_kernel(tc, xT, w1, w2, gate, offs, pos1, pos2
         nc.sync.dma_start(offs_sb[:], offs)
         for j in (0, 1, 3):
             nc.sync.dma_start(out=x_raw[j][:], in_=xv[:, j, :])
-        for q in range(PACK):
+        for q in (1, 0, 2, 3):
             nc.sync.dma_start(out=w1_raw[q][:], in_=w1v[:, :, q * P : (q + 1) * P])
         for b in range(2):
             nc.sync.dma_start(out=w2_raw[b][:], in_=w2v[:, :, b * P : (b + 1) * P])
@@ -59,7 +59,8 @@ def tile_picked_sub_mlp_relu_sub_e_kernel(tc, xT, w1, w2, gate, offs, pos1, pos2
         make_identity(nc, identity[:])
 
         x_got = sb([P, 2, SLICE], F32, "x_got")
-        x_woven = sb([P, 2, 2, P, PACK], BF16, "x_woven")
+        staged = sb([P, 24 * P], BF16, "staged")
+        x_woven = staged[:, 0 : 16 * P].rearrange("p (h s n j) -> p h s n j", h=2, s=2, j=PACK)
         x_pairs = sb([P, 2, SLICE, 2], BF16, "x_pairs")
         x_group = [x_woven[:, :, 1], x_woven[:, :, 0]]
         x_scales = [sb([P, SLICE], U8, f"x_scales{s}") for s in range(SLICES)]
@@ -89,16 +90,18 @@ def tile_picked_sub_mlp_relu_sub_e_kernel(tc, xT, w1, w2, gate, offs, pos1, pos2
         gather_pair(3)
 
         w1_parts = [(0, 64), (64, 96), (96, 128)]
-        w1_part = [sb([P, PACK, b - a, PACK], BF16, f"w1_part{a}") for a, b in w1_parts]
+        head = 16 * P - 32
+        w1_part = [
+            staged[:, head : head + 8 * P].rearrange("p (t m j) -> p t m j", t=PACK, j=PACK),
+            sb([P, PACK, 32, PACK], BF16, "w1_part64")[:],
+            staged[:, head - 2 * P : head + 2 * P].rearrange("p (t m j) -> p t m j", t=PACK, j=PACK),
+        ]
         w1_codes = sb([P, H], U32, "w1_codes")
         w1_scales = sb([P, H], U8, "w1_scales")
 
         def interleave_w1(engine, dst, src):
             engine(dst.rearrange("p t m j -> p m j t"), src.rearrange("p j (m t) -> p m j t", t=PACK))
 
-        for q, dst in enumerate((w1_part[0][:, :, 0:32], w1_part[0][:, :, 32:64], w1_part[1][:])):
-            interleave_w1(nc.scalar.copy, dst, w1_raw[q][:])
-        interleave_w1(nc.scalar.copy, w1_part[2][:, :, 0:16], w1_raw[3][:, :, 0:64])
 
         def quantize_w1(h):
             for t in range(PACK):
@@ -146,14 +149,21 @@ def tile_picked_sub_mlp_relu_sub_e_kernel(tc, xT, w1, w2, gate, offs, pos1, pos2
                     stop=True,
                 )
         gather_into(1, 3)
+        interleave_w1(nc.scalar.copy, w1_part[0][:, :, 32:64], w1_raw[1][:])
+        interleave_w1(nc.scalar.copy, w1_part[0][:, :, 12:32], w1_raw[0][:, :, 48:128])
+        nc.gpsimd.tensor_scalar(
+            w1_part[0][:, :, 0:12], w1_raw[0][:, :, 0:48].rearrange("p j (m t) -> p t m j", t=PACK), 1.0, 0.0, MULT, ADD
+        )
+        interleave_w1(nc.scalar.copy, w1_part[1], w1_raw[2][:])
+        quantize_w1(0)
+        interleave_w1(nc.scalar.copy, w1_part[2][:, :, 0:20], w1_raw[3][:, :, 0:80])
         x_quads = sb([P, 2, P, 2], U32, "w1_raw2")
         nc.scalar.copy(
             x_quads[:].rearrange("p h (c i) u -> p h c u i", i=2),
             x_pairs[:].rearrange("p u n e -> p u (n e)").bitcast(U32).rearrange("p u (h c i) -> p h c u i", h=2, i=2),
         )
         x_group.append(x_quads[:].bitcast(BF16))
-        quantize_w1(0)
-        interleave_w1(nc.vector.tensor_copy, w1_part[2][:, :, 16:32], w1_raw[3][:, :, 64:128])
+        interleave_w1(nc.vector.tensor_copy, w1_part[2][:, :, 20:32], w1_raw[3][:, :, 80:128])
         quantize_w1(1)
         quantize_w1(2)
         quantize_x(1, "w1_raw3")
@@ -248,16 +258,22 @@ def tile_picked_sub_mlp_relu_sub_e_kernel(tc, xT, w1, w2, gate, offs, pos1, pos2
         interleave_w2(nc.vector.tensor_copy, w2_second, 1)
         quantize_w2(w2_second, 1)
 
-        turn = [[sb([P, V], F32, f"turn{b}_{d}") for d in range(D - 1)] for b in range(2)]
-        for b in range(2):
-            turn[b].append(turn[1][b])
+        held = [[sb([P, V], F32, f"turn{b}_{d}") for d in range(D - b)] for b in range(2)]
+
+        def turn(b, d, cols):
+            if (b, d) == (0, 3) and cols.start >= P:
+                return held[1][0][:, cols]
+            if (b, d) == (1, 3):
+                return held[1][1][:, cols]
+            return held[b][d][:, cols]
+
         flipped = [sb([P, V], F32, f"flipped{b}") for b in range(2)]
         result = [sb([P, V], F32, f"result{b}") for b in range(2)]
         pieces = [slice(c * P, (c + 1) * P) for c in range(V // P)]
 
         def fetch(b, d, cols=slice(0, V)):
             places = pos_sb[d][:, cols.start // LANE : cols.stop // LANE]
-            nc.vector.tensor_tensor(turn[b][d][:, cols], y[b][:].indirect(places), gates[:, d, cols], MULT)
+            nc.vector.tensor_tensor(turn(b, d, cols), y[b][:].indirect(places), gates[:, d, cols], MULT)
 
         def store(b, cols):
             nc.sync.dma_start(out=out[b * P : (b + 1) * P, cols], in_=result[b][:, cols])
@@ -272,32 +288,57 @@ def tile_picked_sub_mlp_relu_sub_e_kernel(tc, xT, w1, w2, gate, offs, pos1, pos2
         nc.scalar.copy(y[1][:, 0 : 2 * SLICE], y1_psum[0][:])
         nc.scalar.copy(y[1][:, 2 * SLICE : S], y1_psum[1][:, 0:SLICE])
 
-        def partial_sum(b, sums, backs):
-            for d in range(D - 1):
-                if (b, d) != (0, 0):
-                    fetch(b, d)
-                for c, cols in enumerate(pieces):
-                    flip(sums[c][:], turn[b][d][:, cols], d == 0, d == D - 2)
-            for c, cols in enumerate(pieces):
-                nc.scalar.copy(flipped[b][:, cols], sums[c][:])
-            for c, cols in enumerate(pieces):
-                flip(backs[:, cols], flipped[b][:, cols])
+        def bank(name, width=P):
+            return psum.tile([P, width], F32, name=name, bufs=4 if name == "h_bank" else 1)
 
-        sums0 = [psum.tile([P, P], F32, name=f"y_psum{c}") for c in range(len(pieces))]
-        back0 = psum.tile([P, V], F32, name="h_bank", bufs=4)
-        partial_sum(0, sums0, back0)
-        sums1 = [psum.tile([P, P], F32, name=f"y_psum{c}") for c in range(len(pieces))]
-        back1 = psum.tile([P, V], F32, name="h_bank", bufs=4)
-        partial_sum(1, sums1, back1)
+        sums = [[bank(f"y_psum{c}") for c in range(3)], [bank("y_psum3"), bank("h_bank"), bank("h_bank")]]
+        wide, narrow = slice(0, 2 * P), slice(2 * P, V)
 
-        def finish(b, backs, cols):
-            nc.vector.tensor_tensor(result[b][:, cols], backs[:, cols], turn[b][3][:, cols], ADD)
+        def add_turn(b, d, cols, stop):
+            for c in range(cols.start // P, cols.stop // P):
+                flip(sums[b][c][:], turn(b, d, pieces[c]), d == 0, stop)
+
+        def copy_sums(b, cols):
+            for c in range(cols.start // P, cols.stop // P):
+                nc.scalar.copy(flipped[b][:, pieces[c]], sums[b][c][:])
+
+        def turn_back(b, cols, name):
+            back = bank(name, cols.stop - cols.start)
+            for c in range(cols.start // P, cols.stop // P):
+                flip(back[:, c * P - cols.start : (c + 1) * P - cols.start], flipped[b][:, pieces[c]])
+            return back
+
+        def finish(b, back, cols):
+            nc.vector.tensor_tensor(result[b][:, cols], back[:], turn(b, 3, cols), ADD)
             store(b, cols)
 
-        ends = [slice(0, 256), slice(256, V)]
-        fetch(0, 3)
-        fetch(1, 3, ends[0])
-        finish(0, back0, slice(0, V))
-        fetch(1, 3, ends[1])
-        for cols in ends:
-            finish(1, back1, cols)
+        add_turn(0, 0, slice(0, V), False)
+        fetch(0, 1)
+        add_turn(0, 1, slice(0, V), False)
+        fetch(0, 2)
+        head, rest = slice(0, P), slice(P, V)
+        add_turn(0, 2, head, False)
+        add_turn(0, 2, rest, True)
+        fetch(0, 3, head)
+        add_turn(0, 3, head, True)
+        copy_sums(0, rest)
+        copy_sums(0, head)
+        back0 = turn_back(0, rest, "h_bank")
+        whole = turn_back(0, head, "y_psum2")
+        nc.scalar.copy(result[0][:, head], whole[:])
+        store(0, head)
+        for d in range(2):
+            fetch(1, d)
+            add_turn(1, d, slice(0, V), False)
+        fetch(1, 2)
+        add_turn(1, 2, slice(0, V), True)
+        copy_sums(1, wide)
+        back1 = turn_back(1, wide, "y_psum0")
+        copy_sums(1, narrow)
+        back2 = turn_back(1, narrow, "y_psum1")
+        fetch(0, 3, rest)
+        fetch(1, 3, wide)
+        finish(0, back0, rest)
+        fetch(1, 3, narrow)
+        finish(1, back1, wide)
+        finish(1, back2, narrow)

@@ -19,8 +19,9 @@ COPY = mybir.ActivationFunctionType.Copy
 P = 128
 PACK = 4
 SLICE = 256
-SLICES = S // SLICE
 LANE = 16
+PIECES = V // P
+PLAIN = 3
 
 
 def tile_picked_sub_mlp_relu_sub_e_kernel(tc, xT, w1, w2, gate, offs, pos1, pos2, pos3, pos4, out):
@@ -32,313 +33,222 @@ def tile_picked_sub_mlp_relu_sub_e_kernel(tc, xT, w1, w2, gate, offs, pos1, pos2
         def sb(shape, dtype, name):
             return keep.tile(shape, dtype, name=name, align_bytes=64)
 
+        def bank(number, shape):
+            return psum.tile([P] + shape, F32, name=f"bank{number}")
+
+        def places(lists, cols):
+            return lists[:, cols.start // LANE : cols.stop // LANE]
+
         offs_sb = keep.tile([P, S // LANE], U16, name="offs_sb")
         pos_sb = [keep.tile([P, V // LANE], U16, name=f"pos_sb{d}") for d in range(D)]
-
         x_raw = [sb([P, T], F32, f"x_raw{j}") for j in range(PACK)]
         w1_raw = [sb([P, PACK, P], F32, f"w1_raw{q}") for q in range(PACK)]
         w2_raw = [sb([P, PACK, P], F32, f"w2_raw{b}") for b in range(2)]
         gates = sb([P, D, V], F32, "gates")
+        gate_cols = sb([P, PLAIN, PIECES], F32, "gate_cols")
 
         xv = xT.rearrange("(p j) t -> p j t", j=PACK)
         w1v = w1.rearrange("(p j) c -> p j c", j=PACK)
         w2v = w2.rearrange("(p j) c -> p j c", j=PACK)
-        nc.sync.dma_start(out=x_raw[2][:], in_=xv[:, 2, :])
+        nc.sync.dma_start(out=x_raw[0][:], in_=xv[:, 0, :])
         nc.sync.dma_start(offs_sb[:], offs)
-        for j in (0, 1, 3):
+        for j in range(1, PACK):
             nc.sync.dma_start(out=x_raw[j][:], in_=xv[:, j, :])
-        for q in (1, 0, 2, 3):
+        for q in range(PACK):
             nc.sync.dma_start(out=w1_raw[q][:], in_=w1v[:, :, q * P : (q + 1) * P])
         for b in range(2):
             nc.sync.dma_start(out=w2_raw[b][:], in_=w2v[:, :, b * P : (b + 1) * P])
         nc.sync.dma_start(out=gates[:], in_=gate[:, 0:P, :].rearrange("d p v -> p d v"))
         for d, p in enumerate((pos1, pos2, pos3, pos4)):
             nc.sync.dma_start(pos_sb[d][:], p)
+        thirds = gate.rearrange("d m v -> (d m v)").rearrange("(k r) -> k r", k=D * PIECES)
+        with nc.allow_non_contiguous_dma(reason="one gate value a partition"):
+            nc.sync.dma_start(out=gate_cols[:].rearrange("p d c -> p (d c)"), in_=thirds[0 : PLAIN * PIECES, 0:P].rearrange("k p -> p k"))
 
         identity = sb([P, P], F32, "identity")
         make_identity(nc, identity[:])
 
-        x_got = sb([P, 2, SLICE], F32, "x_got")
-        staged = sb([P, 24 * P], BF16, "staged")
-        x_woven = staged[:, 0 : 16 * P].rearrange("p (h s n j) -> p h s n j", h=2, s=2, j=PACK)
-        x_pairs = sb([P, 2, SLICE, 2], BF16, "x_pairs")
-        x_group = [x_woven[:, :, 1], x_woven[:, :, 0]]
-        x_scales = [sb([P, SLICE], U8, f"x_scales{s}") for s in range(SLICES)]
+        slices = [slice(s * SLICE, (s + 1) * SLICE) for s in range(S // SLICE)]
+        x_woven = [sb([P, SLICE, PACK], BF16, f"x_woven{s}") for s in range(3)]
+        x_codes = [sb([P, SLICE], U32, f"x_codes{s}") for s in range(3)]
+        x_scales = [sb([P, SLICE], U8, f"x_scales{s}") for s in range(3)]
+        flat = sb([P, 3, S], BF16, "flat")
+        flat_mid = sb([P, SLICE], BF16, "flat_mid")
 
-        def entries(s):
-            return offs_sb[:, s * SLICE // LANE : (s + 1) * SLICE // LANE]
+        def gather_flat(dst, j, cols):
+            nc.scalar.activation(dst, x_raw[j][:].indirect(places(offs_sb, cols)), COPY)
 
-        def gather_into(s, j):
-            nc.vector.tensor_copy(x_group[s][:, :, :, j], x_raw[j][:].indirect(entries(s)))
+        def gather_into(dst, j, cols):
+            nc.vector.tensor_copy(dst, x_raw[j][:].indirect(places(offs_sb, cols)))
 
-        def gather_pair(j):
-            nc.vector.tensor_copy(x_pairs[:, j // 2, :, j % 2], x_raw[j][:].indirect(entries(2)))
+        def place(engine, s, planes):
+            engine(x_woven[s][:, :, 0:planes], flat[:, 0:planes, slices[s]].rearrange("p j n -> p n j"))
 
-        for s in range(2):
-            gather_into(s, 2)
-        gather_pair(2)
-        for j in range(2):
-            nc.vector.tensor_copy(x_got[:, j], x_raw[j][:].indirect(entries(0)))
-            if j == 1:
-                for h in range(2):
-                    nc.scalar.copy(
-                        x_group[0][:, h, :, 0:2], x_got[:, :, h * P : (h + 1) * P].rearrange("p j n -> p n j")
-                    )
-            gather_pair(j)
-            gather_into(1, j)
-        gather_into(0, 3)
-        gather_pair(3)
+        def quantize(codes, scales, values):
+            nc.vector.quantize_mx(out=codes.bitcast(FP8X4), scales=scales, in_=values.rearrange("p n j -> p (n j)"))
 
-        w1_parts = [(0, 64), (64, 96), (96, 128)]
-        head = 16 * P - 32
-        w1_part = [
-            staged[:, head : head + 8 * P].rearrange("p (t m j) -> p t m j", t=PACK, j=PACK),
-            sb([P, PACK, 32, PACK], BF16, "w1_part64")[:],
-            staged[:, head - 2 * P : head + 2 * P].rearrange("p (t m j) -> p t m j", t=PACK, j=PACK),
-        ]
+        rest = slice(SLICE, S)
+        gather_into(flat[:, 0, :], 0, slice(0, S))
+        gather_into(flat[:, 1, slices[0]], 1, slices[0])
+        place(nc.scalar.copy, 0, 2)
+        gather_into(flat[:, 1, rest], 1, rest)
+        gather_into(x_woven[0][:, :, 2], 2, slices[0])
+        for s in (1, 2):
+            gather_flat(flat[:, 2, slices[s]], 2, slices[s])
+            place(nc.vector.tensor_copy, s, 3)
+
+        w1_woven = sb([P, PACK, P, PACK], BF16, "w1_woven")
         w1_codes = sb([P, H], U32, "w1_codes")
         w1_scales = sb([P, H], U8, "w1_scales")
 
-        def interleave_w1(engine, dst, src):
-            engine(dst.rearrange("p t m j -> p m j t"), src.rearrange("p j (m t) -> p m j t", t=PACK))
+        def weave_w1(engine, q, m):
+            engine(
+                w1_woven[:, :, 32 * q + m.start : 32 * q + m.stop].rearrange("p t m j -> p m j t"),
+                w1_raw[q][:, :, PACK * m.start : PACK * m.stop].rearrange("p j (m t) -> p m j t", t=PACK),
+            )
 
-
-        def quantize_w1(h):
-            for t in range(PACK):
-                cols = slice(t * P + w1_parts[h][0], t * P + w1_parts[h][1])
-                nc.vector.quantize_mx(
-                    out=w1_codes[:, cols].bitcast(FP8X4),
-                    scales=w1_scales[:, cols],
-                    in_=w1_part[h][:, t].rearrange("p m j -> p (m j)"),
-                )
-
-        x_codes = []
-
-        def quantize_x(s, name):
-            x_codes.append(sb([P, SLICE], U32, name))
-            parts = 2 if s < 2 else 1
-            for h in range(parts):
-                cols = slice(h * SLICE // parts, (h + 1) * SLICE // parts)
-                nc.vector.quantize_mx(
-                    out=x_codes[s][:, cols].bitcast(FP8X4),
-                    scales=x_scales[s][:, cols],
-                    in_=x_group[s][:, h * 2 // parts : (h + 1) * 2 // parts].rearrange("p h n j -> p (h n j)"),
-                )
-
-        quantize_x(0, "x_codes0")
-        y_psum = [psum.tile([P, SLICE], F32, name=f"y_psum{s}") for s in range(SLICES + 1)]
-        nc.tensor.matmul_mx(
-            out=y_psum[3][:, 0:P],
-            lhsT=x_codes[0][:, 0:P].bitcast(FP8X4),
-            lhsT_scale=x_scales[0][:, 0:P],
-            rhs=x_codes[0][:, 0:P].bitcast(FP8X4),
-            rhs_scale=x_scales[0][:, 0:P],
-            start=True,
-            stop=True,
-        )
-        for b in range(2):
-            warm = psum.tile([P, 2, SLICE], F32, name="h_bank", bufs=4)
-            for i in range(2):
-                nc.tensor.matmul_mx(
-                    out=warm[:, i, :],
-                    lhsT=x_codes[0][:, 0:P].bitcast(FP8X4),
-                    lhsT_scale=x_scales[0][:, 0:P],
-                    rhs=x_codes[0][:].bitcast(FP8X4),
-                    rhs_scale=x_scales[0][:],
-                    start=True,
-                    stop=True,
-                )
-        gather_into(1, 3)
-        interleave_w1(nc.scalar.copy, w1_part[0][:, :, 32:64], w1_raw[1][:])
-        interleave_w1(nc.scalar.copy, w1_part[0][:, :, 12:32], w1_raw[0][:, :, 48:128])
-        nc.gpsimd.tensor_scalar(
-            w1_part[0][:, :, 0:12], w1_raw[0][:, :, 0:48].rearrange("p j (m t) -> p t m j", t=PACK), 1.0, 0.0, MULT, ADD
-        )
-        interleave_w1(nc.scalar.copy, w1_part[1], w1_raw[2][:])
-        quantize_w1(0)
-        interleave_w1(nc.scalar.copy, w1_part[2][:, :, 0:20], w1_raw[3][:, :, 0:80])
-        x_quads = sb([P, 2, P, 2], U32, "w1_raw2")
-        nc.scalar.copy(
-            x_quads[:].rearrange("p h (c i) u -> p h c u i", i=2),
-            x_pairs[:].rearrange("p u n e -> p u (n e)").bitcast(U32).rearrange("p u (h c i) -> p h c u i", h=2, i=2),
-        )
-        x_group.append(x_quads[:].bitcast(BF16))
-        interleave_w1(nc.vector.tensor_copy, w1_part[2][:, :, 20:32], w1_raw[3][:, :, 80:128])
-        quantize_w1(1)
-        quantize_w1(2)
-        quantize_x(1, "w1_raw3")
-        quantize_x(2, "x_codes2")
-
+        w2_woven = [sb([P, P, PACK], BF16, f"w2_woven{b}") for b in range(2)]
         w2_codes = [sb([P, P], U32, f"w2_codes{b}") for b in range(2)]
         w2_scales = [sb([P, P], U8, f"w2_scales{b}") for b in range(2)]
 
-        def interleave_w2(engine, group, b):
+        def weave_w2(engine, b):
             engine(
-                group.rearrange("p (c i) j -> p c j i", i=4),
+                w2_woven[b][:].rearrange("p (c i) j -> p c j i", i=4),
                 w2_raw[b][:].rearrange("p j (c i) -> p c j i", i=4),
             )
 
-        def quantize_w2(group, b):
-            nc.vector.quantize_mx(
-                out=w2_codes[b][:].bitcast(FP8X4), scales=w2_scales[b][:], in_=group.rearrange("p n j -> p (n j)")
-            )
+        gather_into(x_woven[0][:, :, 3], 3, slices[0])
+        gather_flat(flat_mid[:], 3, slices[1])
+        weave_w1(nc.scalar.copy, 0, slice(0, 32))
+        nc.vector.tensor_copy(x_woven[1][:, :, 3], flat_mid[:])
+        quantize(x_codes[0][:], x_scales[0][:], x_woven[0][:])
+        weave_w1(nc.scalar.copy, 1, slice(0, 32))
+        quantize(x_codes[1][:], x_scales[1][:], x_woven[1][:])
+        weave_w1(nc.scalar.copy, 2, slice(0, 12))
+        weave_w1(nc.vector.tensor_copy, 2, slice(12, 32))
+        weave_w1(nc.vector.tensor_copy, 3, slice(12, 32))
+        weave_w1(nc.scalar.copy, 3, slice(0, 12))
+        flat_last = sb([P, SLICE], BF16, "w1_raw3")
+        gather_flat(flat_last[:], 3, slices[2])
+        for t in range(PACK):
+            tile_t = slice(t * P, (t + 1) * P)
+            quantize(w1_codes[:, tile_t], w1_scales[:, tile_t], w1_woven[:, t])
+        weave_w2(nc.scalar.copy, 0)
+        weave_w2(nc.vector.tensor_copy, 1)
+        nc.vector.tensor_copy(x_woven[2][:, :, 3], flat_last[:])
+        quantize(w2_codes[0][:], w2_scales[0][:], w2_woven[0][:])
+        quantize(x_codes[2][:], x_scales[2][:], x_woven[2][:])
+        quantize(w2_codes[1][:], w2_scales[1][:], w2_woven[1][:])
 
-        h_group = [sb([P, SLICE, PACK], BF16, f"h_group{s}") for s in range(SLICES)]
-        h_codes = [sb([P, SLICE], U32, f"h_codes{s}") for s in range(SLICES)]
-        h_scales = [sb([P, SLICE], U8, f"h_scales{s}") for s in range(SLICES)]
+        h_woven = [sb([P, SLICE, PACK], BF16, f"h_woven{s}") for s in range(3)]
+        h_codes = [sb([P, SLICE], U32, f"h_codes{s}") for s in range(3)]
+        h_scales = [sb([P, SLICE], U8, f"h_scales{s}") for s in range(3)]
+        y = [sb([P, S], F32, f"y{b}") for b in range(2)]
 
-        def first(s, half, engine, parts=1):
-            bank = psum.tile([P, PACK, P], F32, name="h_bank", bufs=4)
-            cols = slice(half * P, (half + 1) * P)
-            for t in range(PACK):
-                nc.tensor.matmul_mx(
-                    out=bank[:, t, :],
-                    lhsT=w1_codes[:, t * P : (t + 1) * P].bitcast(FP8X4),
-                    lhsT_scale=w1_scales[:, t * P : (t + 1) * P],
-                    rhs=x_codes[s][:, cols].bitcast(FP8X4),
-                    rhs_scale=x_scales[s][:, cols],
-                    start=True,
-                    stop=True,
-                )
-            dst = h_group[s][:, cols, :].rearrange("p (c i) t -> p c t i", i=2)
-            src = bank[:].rearrange("p t (c i) -> p c t i", i=2)
-            for k in range(parts):
-                pairs = slice(k * P // 2 // parts, (k + 1) * P // 2 // parts)
-                if engine == "scalar":
-                    nc.scalar.activation(dst[:, pairs], src[:, pairs], RELU)
-                else:
-                    nc.vector.tensor_scalar_max(dst[:, pairs], src[:, pairs], 0.0)
-
-        def quantize_h(s, cols=slice(0, SLICE)):
-            nc.vector.quantize_mx(
-                out=h_codes[s][:, cols].bitcast(FP8X4),
-                scales=h_scales[s][:, cols],
-                in_=h_group[s][:, cols, :].rearrange("p n j -> p (n j)"),
-            )
-
-        def second(dst, b, s, cols=slice(0, SLICE)):
+        def product(dst, w_codes, w_scales, codes, scales):
             nc.tensor.matmul_mx(
                 out=dst,
-                lhsT=w2_codes[b][:].bitcast(FP8X4),
-                lhsT_scale=w2_scales[b][:],
-                rhs=h_codes[s][:, cols].bitcast(FP8X4),
-                rhs_scale=h_scales[s][:, cols],
+                lhsT=w_codes.bitcast(FP8X4),
+                lhsT_scale=w_scales,
+                rhs=codes.bitcast(FP8X4),
+                rhs_scale=scales,
                 start=True,
                 stop=True,
             )
 
-        y = [sb([P, S], F32, f"y{b}") for b in range(2)]
-        w2_first = sb([P, P, PACK], BF16, "w1_raw2")
-        halves = [slice(0, P), slice(P, SLICE)]
+        def first(number, s, cols):
+            sums = bank(number, [PACK, cols.stop - cols.start])
+            for t in range(PACK):
+                tile_t = slice(t * P, (t + 1) * P)
+                product(sums[:, t, :], w1_codes[:, tile_t], w1_scales[:, tile_t], x_codes[s][:, cols], x_scales[s][:, cols])
+            return sums
 
-        nc.gpsimd.tensor_scalar(w2_first[:], w2_raw[0][:].rearrange("p j n -> p n j"), 1.0, 0.0, MULT, ADD)
-        first(0, 0, "scalar")
-        first(0, 1, "vector")
-        first(1, 0, "scalar")
-        first(1, 1, "vector")
-        quantize_w2(w2_first[:], 0)
-        quantize_h(0)
-        first(2, 0, "scalar")
-        first(2, 1, "scalar", 2)
-        second(y_psum[0][:], 0, 0)
-        quantize_h(1)
-        second(y_psum[1][:], 0, 1)
-        nc.scalar.copy(y[0][:, SLICE : 2 * SLICE], y_psum[1][:])
-        quantize_h(2, halves[0])
-        second(y_psum[3][:, 0:P], 0, 2, halves[0])
-        nc.scalar.copy(y[0][:, 2 * SLICE : 2 * SLICE + P], y_psum[3][:, 0:P])
-        nc.vector.tensor_copy(y[0][:, 0:SLICE], y_psum[0][:])
-        last_bank = psum.tile([P, P // 2], F32, name="h_bank", bufs=4)
-        for k, bank in enumerate((y_psum[2][:, 0 : P // 2], last_bank[:])):
-            cols = slice(P + k * P // 2, P + (k + 1) * P // 2)
-            quantize_h(2, cols)
-            second(bank, 0, 2, cols)
-            nc.scalar.copy(y[0][:, 2 * SLICE + cols.start : 2 * SLICE + cols.stop], bank)
-        w2_second = h_group[2][:, 0:P, :]
-        interleave_w2(nc.vector.tensor_copy, w2_second, 1)
-        quantize_w2(w2_second, 1)
+        def relu(on_scalar, sums, s, cols):
+            dst = h_woven[s][:, cols, :].rearrange("p (c i) t -> p c t i", i=2)
+            src = sums[:].rearrange("p t (c i) -> p c t i", i=2)
+            if on_scalar:
+                nc.scalar.activation(dst, src, RELU)
+            else:
+                nc.vector.tensor_scalar_max(dst, src, 0.0)
 
-        held = [[sb([P, V], F32, f"turn{b}_{d}") for d in range(D - b)] for b in range(2)]
+        def quantize_h(s, cols):
+            quantize(h_codes[s][:, cols], h_scales[s][:, cols], h_woven[s][:, cols, :])
 
-        def turn(b, d, cols):
-            if (b, d) == (0, 3) and cols.start >= P:
-                return held[1][0][:, cols]
-            if (b, d) == (1, 3):
-                return held[1][1][:, cols]
-            return held[b][d][:, cols]
+        def second(dst, b, s, cols):
+            product(dst, w2_codes[b][:], w2_scales[b][:], h_codes[s][:, cols], h_scales[s][:, cols])
 
-        flipped = [sb([P, V], F32, f"flipped{b}") for b in range(2)]
+        whole, left, right = slice(0, SLICE), slice(0, P), slice(P, SLICE)
+
+        relu(True, first(0, 0, left), 0, left)
+        relu(False, first(1, 0, right), 0, right)
+        relu(True, first(2, 1, left), 1, left)
+        quantize_h(0, whole)
+        relu(True, first(3, 1, right), 1, right)
+        relu(False, first(4, 2, left), 2, left)
+        relu(True, first(5, 2, right), 2, right)
+        quantize_h(1, whole)
+        quantize_h(2, left)
+        y_early = [bank(6, [SLICE]), bank(7, [SLICE + P]), bank(0, [2 * SLICE])]
+        second(y_early[0][:], 0, 0, whole)
+        second(y_early[1][:, 0:SLICE], 0, 1, whole)
+        second(y_early[1][:, SLICE:], 0, 2, left)
+        second(y_early[2][:, 0:SLICE], 1, 0, whole)
+        second(y_early[2][:, SLICE:], 1, 1, whole)
+        nc.vector.tensor_copy(y[0][:, 0:SLICE], y_early[0][:])
+        quantize_h(2, right)
+        y_late = [bank(1, [P]), bank(2, [SLICE])]
+        second(y_late[1][:, left], 1, 2, left)
+        second(y_late[0][:], 0, 2, right)
+        second(y_late[1][:, right], 1, 2, right)
+        nc.vector.tensor_copy(y[0][:, SLICE : S - P], y_early[1][:])
+        nc.scalar.copy(y[1][:, 0 : 2 * SLICE], y_early[2][:])
+        nc.vector.tensor_copy(y[0][:, S - P : S], y_late[0][:])
+        nc.scalar.copy(y[1][:, 2 * SLICE : S], y_late[1][:])
+
+        pieces = [slice(c * P, (c + 1) * P) for c in range(PIECES)]
+        gated = [sb([P, V], F32, f"gated{d}") for d in range(D)]
+        gated_last = sb([P, V], F32, "gated_last")
+        plain = [sb([P, V], F32, f"plain{d}") for d in range(PLAIN)]
+        scaled = [sb([P, V], F32, f"scaled{d}") for d in range(PLAIN)]
+        summed = sb([P, V], F32, "summed")
         result = [sb([P, V], F32, f"result{b}") for b in range(2)]
-        pieces = [slice(c * P, (c + 1) * P) for c in range(V // P)]
 
-        def fetch(b, d, cols=slice(0, V)):
-            places = pos_sb[d][:, cols.start // LANE : cols.stop // LANE]
-            nc.vector.tensor_tensor(turn(b, d, cols), y[b][:].indirect(places), gates[:, d, cols], MULT)
+        def fetch_gated(dst, b, d):
+            nc.vector.tensor_tensor(dst[:], y[b][:].indirect(pos_sb[d][:]), gates[:, d, :], MULT)
 
-        def store(b, cols):
+        def flip(dst, src, start, stop):
+            nc.tensor.matmul(dst, src, identity[:], start=start, stop=stop, is_transpose=True)
+
+        def finish(b, back, last_turn, cols):
+            nc.vector.tensor_tensor(result[b][:, cols], back, last_turn[:, cols], ADD)
             nc.sync.dma_start(out=out[b * P : (b + 1) * P, cols], in_=result[b][:, cols])
 
-        def flip(bank, src, start=True, stop=True):
-            nc.tensor.matmul(bank, src, identity[:], start=start, stop=stop, is_transpose=True)
+        sums0 = bank(4, [V])
+        turned = [bank(5 + d, [V]) for d in range(PLAIN)]
+        for d in range(PLAIN):
+            fetch_gated(gated[d], 0, d)
+            nc.scalar.activation(plain[d][:], y[1][:].indirect(pos_sb[d][:]), COPY)
+            for c in range(PIECES):
+                flip(turned[d][:, pieces[c]], plain[d][:, pieces[c]], True, True)
+            for c in range(PIECES):
+                flip(sums0[:, pieces[c]], gated[d][:, pieces[c]], (d, c) == (0, 0), (d, c) == (PLAIN - 1, PIECES - 1))
+        fetch_gated(gated[3], 0, 3)
+        fetch_gated(gated_last, 1, 3)
 
-        fetch(0, 0)
-        y1_psum = [psum.tile([P, 2 * SLICE], F32, name="h_bank", bufs=4) for i in range(2)]
-        for s in range(SLICES):
-            second(y1_psum[s // 2][:, s % 2 * SLICE : (s % 2 + 1) * SLICE], 1, s)
-        nc.scalar.copy(y[1][:, 0 : 2 * SLICE], y1_psum[0][:])
-        nc.scalar.copy(y[1][:, 2 * SLICE : S], y1_psum[1][:, 0:SLICE])
+        def scale(d, c):
+            nc.scalar.activation(scaled[d][:, pieces[c]], turned[d][:, pieces[c]], COPY, scale=gate_cols[:, d, c : c + 1])
 
-        def bank(name, width=P):
-            return psum.tile([P, width], F32, name=name, bufs=4 if name == "h_bank" else 1)
-
-        sums = [[bank(f"y_psum{c}") for c in range(3)], [bank("y_psum3"), bank("h_bank"), bank("h_bank")]]
-        wide, narrow = slice(0, 2 * P), slice(2 * P, V)
-
-        def add_turn(b, d, cols, stop):
-            for c in range(cols.start // P, cols.stop // P):
-                flip(sums[b][c][:], turn(b, d, pieces[c]), d == 0, stop)
-
-        def copy_sums(b, cols):
-            for c in range(cols.start // P, cols.stop // P):
-                nc.scalar.copy(flipped[b][:, pieces[c]], sums[b][c][:])
-
-        def turn_back(b, cols, name):
-            back = bank(name, cols.stop - cols.start)
-            for c in range(cols.start // P, cols.stop // P):
-                flip(back[:, c * P - cols.start : (c + 1) * P - cols.start], flipped[b][:, pieces[c]])
-            return back
-
-        def finish(b, back, cols):
-            nc.vector.tensor_tensor(result[b][:, cols], back[:], turn(b, 3, cols), ADD)
-            store(b, cols)
-
-        add_turn(0, 0, slice(0, V), False)
-        fetch(0, 1)
-        add_turn(0, 1, slice(0, V), False)
-        fetch(0, 2)
-        head, rest = slice(0, P), slice(P, V)
-        add_turn(0, 2, head, False)
-        add_turn(0, 2, rest, True)
-        fetch(0, 3, head)
-        add_turn(0, 3, head, True)
-        copy_sums(0, rest)
-        copy_sums(0, head)
-        back0 = turn_back(0, rest, "h_bank")
-        whole = turn_back(0, head, "y_psum2")
-        nc.scalar.copy(result[0][:, head], whole[:])
-        store(0, head)
-        for d in range(2):
-            fetch(1, d)
-            add_turn(1, d, slice(0, V), False)
-        fetch(1, 2)
-        add_turn(1, 2, slice(0, V), True)
-        copy_sums(1, wide)
-        back1 = turn_back(1, wide, "y_psum0")
-        copy_sums(1, narrow)
-        back2 = turn_back(1, narrow, "y_psum1")
-        fetch(0, 3, rest)
-        fetch(1, 3, wide)
-        finish(0, back0, rest)
-        fetch(1, 3, narrow)
-        finish(1, back1, wide)
-        finish(1, back2, narrow)
+        for c in range(PIECES):
+            scale(0, c)
+        nc.scalar.copy(summed[:], sums0[:])
+        back0 = bank(0, [V])
+        for c in range(PIECES):
+            flip(back0[:, pieces[c]], summed[:, pieces[c]], True, True)
+        finish(0, back0[:], gated[3], slice(0, V))
+        for c in range(PIECES):
+            for d in range(1, PLAIN):
+                scale(d, c)
+            back1 = bank(1 + c, [P])
+            for d in range(PLAIN):
+                flip(back1[:], scaled[d][:, pieces[c]], d == 0, d == PLAIN - 1)
+            finish(1, back1[:], gated_last, pieces[c])

@@ -213,8 +213,8 @@ def tile_picked_sub_mlp_relu_sub_e_kernel(tc, xT, w1, w2, gate, offs, pos1, pos2
         summed = sb([P, V], F32, "summed")
         result = [sb([P, V], F32, f"result{b}") for b in range(2)]
 
-        def fetch_gated(dst, b, d):
-            nc.vector.tensor_tensor(dst[:], y[b][:].indirect(pos_sb[d][:]), gates[:, d, :], MULT)
+        def fetch_gated(dst, b, d, cols=slice(0, V)):
+            nc.vector.tensor_tensor(dst[:, cols], y[b][:].indirect(places(pos_sb[d], cols)), gates[:, d, cols], MULT)
 
         def flip(dst, src, start, stop):
             nc.tensor.matmul(dst, src, identity[:], start=start, stop=stop, is_transpose=True)
@@ -230,10 +230,13 @@ def tile_picked_sub_mlp_relu_sub_e_kernel(tc, xT, w1, w2, gate, offs, pos1, pos2
             nc.scalar.activation(plain[d][:], y[1][:].indirect(pos_sb[d][:]), COPY)
             for c in range(PIECES):
                 flip(turned[d][:, pieces[c]], plain[d][:, pieces[c]], True, True)
-            for c in range(PIECES):
-                flip(sums0[:, pieces[c]], gated[d][:, pieces[c]], (d, c) == (0, 0), (d, c) == (PLAIN - 1, PIECES - 1))
+            for c in range(PIECES if d < 2 else 0):
+                flip(sums0[:, pieces[c]], gated[d][:, pieces[c]], (d, c) == (0, 0), (d, c) == (1, PIECES - 1))
         fetch_gated(gated[3], 0, 3)
-        fetch_gated(gated_last, 1, 3)
+        fetch_gated(gated_last, 1, 3, slice(0, 2 * P))
+        pair = sb([P, V], F32, "pair")
+        nc.vector.tensor_tensor(pair[:], gated[2][:], gated[3][:], ADD)
+        fetch_gated(gated_last, 1, 3, slice(2 * P, V))
 
         def scale(d, c):
             nc.scalar.activation(scaled[d][:, pieces[c]], turned[d][:, pieces[c]], COPY, scale=gate_cols[:, d, c : c + 1])
@@ -244,7 +247,7 @@ def tile_picked_sub_mlp_relu_sub_e_kernel(tc, xT, w1, w2, gate, offs, pos1, pos2
         back0 = bank(0, [V])
         for c in range(PIECES):
             flip(back0[:, pieces[c]], summed[:, pieces[c]], True, True)
-        finish(0, back0[:], gated[3], slice(0, V))
+        finish(0, back0[:], pair, slice(0, V))
         for c in range(PIECES):
             for d in range(1, PLAIN):
                 scale(d, c)

@@ -28,6 +28,7 @@ def tile_picked_sub_mlp_relu_sub_e_kernel(tc, xT, w1, w2, gate, offs, pos1, pos2
     nc = tc.nc
     with ExitStack() as ctx:
         keep = ctx.enter_context(tc.tile_pool(name="keep", bufs=1))
+        reused = ctx.enter_context(tc.tile_pool(name="reused", bufs=1))
         psum = ctx.enter_context(tc.psum_pool(name="psum", bufs=1))
 
         def sb(shape, dtype, name):
@@ -42,7 +43,8 @@ def tile_picked_sub_mlp_relu_sub_e_kernel(tc, xT, w1, w2, gate, offs, pos1, pos2
         offs_sb = keep.tile([P, S // LANE], U16, name="offs_sb")
         pos_sb = [keep.tile([P, V // LANE], U16, name=f"pos_sb{d}") for d in range(D)]
         x_raw = [sb([P, T], F32, f"x_raw{j}") for j in range(PACK)]
-        w1_raw = [sb([P, PACK, P], F32, f"w1_raw{q}") for q in range(PACK)]
+        w1_raw = [sb([P, PACK, P], F32, f"w1_raw{q}") for q in range(PACK - 1)]
+        w1_raw.append(reused.tile([P, PACK, P], F32, name="w1_last", offset=0, align_bytes=64))
         w2_raw = [sb([P, PACK, P], F32, f"w2_raw{b}") for b in range(2)]
         gates = sb([P, D, V], F32, "gates")
         gate_cols = sb([P, PLAIN, PIECES], F32, "gate_cols")
@@ -70,10 +72,11 @@ def tile_picked_sub_mlp_relu_sub_e_kernel(tc, xT, w1, w2, gate, offs, pos1, pos2
 
         slices = [slice(s * SLICE, (s + 1) * SLICE) for s in range(S // SLICE)]
         x_woven = [sb([P, SLICE, PACK], BF16, f"x_woven{s}") for s in range(3)]
-        x_codes = [sb([P, SLICE], U32, f"x_codes{s}") for s in range(3)]
+        x_codes = [sb([P, SLICE], U32, f"x_codes{s}") for s in (0, 2)]
         x_scales = [sb([P, SLICE], U8, f"x_scales{s}") for s in range(3)]
-        flat = sb([P, 3, S], BF16, "flat")
-        flat_mid = sb([P, SLICE], BF16, "flat_mid")
+        flat = sb([P, 2, S], BF16, "flat")
+        flat_mid = sb([P, 2, SLICE], BF16, "flat_mid")
+        flat_end = sb([P, SLICE], BF16, "flat_end")
 
         def gather_flat(dst, j, cols):
             nc.scalar.activation(dst, x_raw[j][:].indirect(places(offs_sb, cols)), COPY)
@@ -81,8 +84,8 @@ def tile_picked_sub_mlp_relu_sub_e_kernel(tc, xT, w1, w2, gate, offs, pos1, pos2
         def gather_into(dst, j, cols):
             nc.vector.tensor_copy(dst, x_raw[j][:].indirect(places(offs_sb, cols)))
 
-        def place(engine, s, planes):
-            engine(x_woven[s][:, :, 0:planes], flat[:, 0:planes, slices[s]].rearrange("p j n -> p n j"))
+        def place(engine, s, first, pair):
+            engine(x_woven[s][:, :, first : first + 2], pair.rearrange("p j n -> p n j"))
 
         def quantize(codes, scales, values):
             nc.vector.quantize_mx(out=codes.bitcast(FP8X4), scales=scales, in_=values.rearrange("p n j -> p (n j)"))
@@ -90,12 +93,14 @@ def tile_picked_sub_mlp_relu_sub_e_kernel(tc, xT, w1, w2, gate, offs, pos1, pos2
         rest = slice(SLICE, S)
         gather_into(flat[:, 0, :], 0, slice(0, S))
         gather_into(flat[:, 1, slices[0]], 1, slices[0])
-        place(nc.scalar.copy, 0, 2)
+        place(nc.scalar.copy, 0, 0, flat[:, :, slices[0]])
         gather_into(flat[:, 1, rest], 1, rest)
-        gather_into(x_woven[0][:, :, 2], 2, slices[0])
         for s in (1, 2):
-            gather_flat(flat[:, 2, slices[s]], 2, slices[s])
-            place(nc.vector.tensor_copy, s, 3)
+            place(nc.vector.tensor_copy, s, 0, flat[:, :, slices[s]])
+        gather_into(x_woven[0][:, :, 2], 2, slices[0])
+        gather_flat(flat_end[:], 2, slices[2])
+        gather_flat(flat_mid[:, 0], 2, slices[1])
+        nc.vector.tensor_copy(x_woven[2][:, :, 2], flat_end[:])
 
         w1_woven = sb([P, PACK, P, PACK], BF16, "w1_woven")
         w1_codes = sb([P, H], U32, "w1_codes")
@@ -118,21 +123,21 @@ def tile_picked_sub_mlp_relu_sub_e_kernel(tc, xT, w1, w2, gate, offs, pos1, pos2
             )
 
         gather_into(x_woven[0][:, :, 3], 3, slices[0])
-        gather_flat(flat_mid[:], 3, slices[1])
+        gather_flat(flat_mid[:, 1], 3, slices[1])
         weave_w1(nc.scalar.copy, 0, slice(0, 32))
-        nc.vector.tensor_copy(x_woven[1][:, :, 3], flat_mid[:])
+        place(nc.vector.tensor_copy, 1, 2, flat_mid[:])
         quantize(x_codes[0][:], x_scales[0][:], x_woven[0][:])
         weave_w1(nc.scalar.copy, 1, slice(0, 32))
-        quantize(x_codes[1][:], x_scales[1][:], x_woven[1][:])
-        weave_w1(nc.scalar.copy, 2, slice(0, 12))
-        weave_w1(nc.vector.tensor_copy, 2, slice(12, 32))
+        weave_w1(nc.vector.tensor_copy, 2, slice(0, 32))
         weave_w1(nc.vector.tensor_copy, 3, slice(12, 32))
         weave_w1(nc.scalar.copy, 3, slice(0, 12))
-        flat_last = sb([P, SLICE], BF16, "w1_raw3")
+        flat_last = reused.tile([P, SLICE], BF16, name="flat_last", offset=0, align_bytes=64)
         gather_flat(flat_last[:], 3, slices[2])
         for t in range(PACK):
             tile_t = slice(t * P, (t + 1) * P)
             quantize(w1_codes[:, tile_t], w1_scales[:, tile_t], w1_woven[:, t])
+        x_codes.insert(1, reused.tile([P, SLICE], U32, name="x_codes1", offset=1024, align_bytes=64))
+        quantize(x_codes[1][:], x_scales[1][:], x_woven[1][:])
         weave_w2(nc.scalar.copy, 0)
         weave_w2(nc.vector.tensor_copy, 1)
         nc.vector.tensor_copy(x_woven[2][:, :, 3], flat_last[:])

@@ -72,11 +72,10 @@ def tile_picked_sub_mlp_relu_sub_e_kernel(tc, xT, w1, w2, gate, offs, pos1, pos2
 
         slices = [slice(s * SLICE, (s + 1) * SLICE) for s in range(S // SLICE)]
         x_woven = [sb([P, SLICE, PACK], BF16, f"x_woven{s}") for s in range(3)]
-        x_codes = [sb([P, SLICE], U32, f"x_codes{s}") for s in (0, 2)]
+        x_codes = [sb([P, SLICE], U32, "x_codes0")]
         x_scales = [sb([P, SLICE], U8, f"x_scales{s}") for s in range(3)]
-        flat = sb([P, 2, S], BF16, "flat")
-        flat_mid = sb([P, 2, SLICE], BF16, "flat_mid")
-        flat_end = sb([P, SLICE], BF16, "flat_end")
+        flat = sb([P, 3, S], BF16, "flat")
+        flat_last = [None] + [sb([P, SLICE], BF16, f"flat_last{s}") for s in (1, 2)]
 
         def gather_flat(dst, j, cols):
             nc.scalar.activation(dst, x_raw[j][:].indirect(places(offs_sb, cols)), COPY)
@@ -84,8 +83,8 @@ def tile_picked_sub_mlp_relu_sub_e_kernel(tc, xT, w1, w2, gate, offs, pos1, pos2
         def gather_into(dst, j, cols):
             nc.vector.tensor_copy(dst, x_raw[j][:].indirect(places(offs_sb, cols)))
 
-        def place(engine, s, first, pair):
-            engine(x_woven[s][:, :, first : first + 2], pair.rearrange("p j n -> p n j"))
+        def place(engine, s, planes):
+            engine(x_woven[s][:, :, 0:planes], flat[:, 0:planes, slices[s]].rearrange("p j n -> p n j"))
 
         def quantize(codes, scales, values):
             nc.vector.quantize_mx(out=codes.bitcast(FP8X4), scales=scales, in_=values.rearrange("p n j -> p (n j)"))
@@ -93,14 +92,12 @@ def tile_picked_sub_mlp_relu_sub_e_kernel(tc, xT, w1, w2, gate, offs, pos1, pos2
         rest = slice(SLICE, S)
         gather_into(flat[:, 0, :], 0, slice(0, S))
         gather_into(flat[:, 1, slices[0]], 1, slices[0])
-        place(nc.scalar.copy, 0, 0, flat[:, :, slices[0]])
+        place(nc.scalar.copy, 0, 2)
         gather_into(flat[:, 1, rest], 1, rest)
-        for s in (1, 2):
-            place(nc.vector.tensor_copy, s, 0, flat[:, :, slices[s]])
         gather_into(x_woven[0][:, :, 2], 2, slices[0])
-        gather_flat(flat_end[:], 2, slices[2])
-        gather_flat(flat_mid[:, 0], 2, slices[1])
-        nc.vector.tensor_copy(x_woven[2][:, :, 2], flat_end[:])
+        for s in (1, 2):
+            gather_flat(flat[:, 2, slices[s]], 2, slices[s])
+            place(nc.vector.tensor_copy, s, 3)
 
         w1_woven = sb([P, PACK, P, PACK], BF16, "w1_woven")
         w1_codes = sb([P, H], U32, "w1_codes")
@@ -123,27 +120,25 @@ def tile_picked_sub_mlp_relu_sub_e_kernel(tc, xT, w1, w2, gate, offs, pos1, pos2
             )
 
         gather_into(x_woven[0][:, :, 3], 3, slices[0])
-        gather_flat(flat_mid[:, 1], 3, slices[1])
-        weave_w1(nc.scalar.copy, 0, slice(0, 32))
-        place(nc.vector.tensor_copy, 1, 2, flat_mid[:])
+        for s in (1, 2):
+            gather_flat(flat_last[s][:], 3, slices[s])
+        nc.vector.tensor_copy(x_woven[1][:, :, 3], flat_last[1][:])
         quantize(x_codes[0][:], x_scales[0][:], x_woven[0][:])
+        nc.vector.tensor_copy(x_woven[2][:, :, 3], flat_last[2][:])
+        weave_w1(nc.scalar.copy, 0, slice(0, 32))
         weave_w1(nc.scalar.copy, 1, slice(0, 32))
         weave_w1(nc.vector.tensor_copy, 2, slice(0, 32))
         weave_w1(nc.vector.tensor_copy, 3, slice(12, 32))
         weave_w1(nc.scalar.copy, 3, slice(0, 12))
-        flat_last = reused.tile([P, SLICE], BF16, name="flat_last", offset=0, align_bytes=64)
-        gather_flat(flat_last[:], 3, slices[2])
         for t in range(PACK):
             tile_t = slice(t * P, (t + 1) * P)
             quantize(w1_codes[:, tile_t], w1_scales[:, tile_t], w1_woven[:, t])
-        x_codes.insert(1, reused.tile([P, SLICE], U32, name="x_codes1", offset=1024, align_bytes=64))
-        quantize(x_codes[1][:], x_scales[1][:], x_woven[1][:])
-        weave_w2(nc.scalar.copy, 0)
-        weave_w2(nc.vector.tensor_copy, 1)
-        nc.vector.tensor_copy(x_woven[2][:, :, 3], flat_last[:])
-        quantize(w2_codes[0][:], w2_scales[0][:], w2_woven[0][:])
-        quantize(x_codes[2][:], x_scales[2][:], x_woven[2][:])
-        quantize(w2_codes[1][:], w2_scales[1][:], w2_woven[1][:])
+        for s in (1, 2):
+            x_codes.append(reused.tile([P, SLICE], U32, name=f"x_codes{s}", offset=(s - 1) * 1024, align_bytes=64))
+            quantize(x_codes[s][:], x_scales[s][:], x_woven[s][:])
+        for b in range(2):
+            weave_w2(nc.scalar.copy, b)
+            quantize(w2_codes[b][:], w2_scales[b][:], w2_woven[b][:])
 
         h_woven = [sb([P, SLICE, PACK], BF16, f"h_woven{s}") for s in range(3)]
         h_codes = [sb([P, SLICE], U32, f"h_codes{s}") for s in range(3)]
@@ -230,14 +225,16 @@ def tile_picked_sub_mlp_relu_sub_e_kernel(tc, xT, w1, w2, gate, offs, pos1, pos2
 
         sums0 = bank(4, [V])
         turned = [bank(5 + d, [V]) for d in range(PLAIN)]
-        for d in range(PLAIN):
+        for d in range(2):
             fetch_gated(gated[d], 0, d)
+            for c in range(PIECES):
+                flip(sums0[:, pieces[c]], gated[d][:, pieces[c]], (d, c) == (0, 0), (d, c) == (1, PIECES - 1))
+        for d in range(PLAIN):
             nc.scalar.activation(plain[d][:], y[1][:].indirect(pos_sb[d][:]), COPY)
             for c in range(PIECES):
                 flip(turned[d][:, pieces[c]], plain[d][:, pieces[c]], True, True)
-            for c in range(PIECES if d < 2 else 0):
-                flip(sums0[:, pieces[c]], gated[d][:, pieces[c]], (d, c) == (0, 0), (d, c) == (1, PIECES - 1))
-        fetch_gated(gated[3], 0, 3)
+        for d in range(2, D):
+            fetch_gated(gated[d], 0, d)
         fetch_gated(gated_last, 1, 3, slice(0, 2 * P))
         pair = sb([P, V], F32, "pair")
         nc.vector.tensor_tensor(pair[:], gated[2][:], gated[3][:], ADD)
@@ -246,9 +243,9 @@ def tile_picked_sub_mlp_relu_sub_e_kernel(tc, xT, w1, w2, gate, offs, pos1, pos2
         def scale(d, c):
             nc.scalar.activation(scaled[d][:, pieces[c]], turned[d][:, pieces[c]], COPY, scale=gate_cols[:, d, c : c + 1])
 
+        nc.scalar.copy(summed[:], sums0[:])
         for c in range(PIECES):
             scale(0, c)
-        nc.scalar.copy(summed[:], sums0[:])
         back0 = bank(0, [V])
         for c in range(PIECES):
             flip(back0[:, pieces[c]], summed[:, pieces[c]], True, True)

@@ -72,7 +72,7 @@ def tile_picked_sub_mlp_relu_sub_e_kernel(tc, xT, w1, w2, gate, offs, pos1, pos2
 
         slices = [slice(s * SLICE, (s + 1) * SLICE) for s in range(S // SLICE)]
         x_woven = [sb([P, SLICE, PACK], BF16, f"x_woven{s}") for s in range(3)]
-        x_codes = [sb([P, SLICE], U32, "x_codes0")]
+        x_codes = []
         x_scales = [sb([P, SLICE], U8, f"x_scales{s}") for s in range(3)]
         flat = sb([P, 3, S], BF16, "flat")
         flat_last = [None] + [sb([P, SLICE], BF16, f"flat_last{s}") for s in (1, 2)]
@@ -123,8 +123,9 @@ def tile_picked_sub_mlp_relu_sub_e_kernel(tc, xT, w1, w2, gate, offs, pos1, pos2
         for s in (1, 2):
             gather_flat(flat_last[s][:], 3, slices[s])
         nc.vector.tensor_copy(x_woven[1][:, :, 3], flat_last[1][:])
-        quantize(x_codes[0][:], x_scales[0][:], x_woven[0][:])
         nc.vector.tensor_copy(x_woven[2][:, :, 3], flat_last[2][:])
+        x_codes.append(sb([P, SLICE], U32, "flat_last2"))
+        quantize(x_codes[0][:], x_scales[0][:], x_woven[0][:])
         weave_w1(nc.scalar.copy, 0, slice(0, 32))
         weave_w1(nc.scalar.copy, 1, slice(0, 32))
         weave_w1(nc.vector.tensor_copy, 2, slice(0, 32))
@@ -178,6 +179,12 @@ def tile_picked_sub_mlp_relu_sub_e_kernel(tc, xT, w1, w2, gate, offs, pos1, pos2
             product(dst, w2_codes[b][:], w2_scales[b][:], h_codes[s][:, cols], h_scales[s][:, cols])
 
         whole, left, right = slice(0, SLICE), slice(0, P), slice(P, SLICE)
+
+        unread = bank(7, [2 * SLICE])
+        at = 0
+        for width in (256, 128, 64):
+            product(unread[:, at : at + width], x_codes[0][:, left], x_scales[0][:, left], x_codes[0][:, 0:width], x_scales[0][:, 0:width])
+            at = at + width
 
         relu(True, first(0, 0, left), 0, left)
         relu(False, first(1, 0, right), 0, right)

@@ -144,7 +144,6 @@ def tile_picked_sub_mlp_relu_sub_e_kernel(tc, xT, w1, w2, gate, offs, pos1, pos2
         h_woven = [sb([P, SLICE, PACK], BF16, f"h_woven{s}") for s in range(3)]
         h_codes = [sb([P, SLICE], U32, f"h_codes{s}") for s in range(3)]
         h_scales = [sb([P, SLICE], U8, f"h_scales{s}") for s in range(3)]
-        y = [sb([P, S], F32, f"y{b}") for b in range(2)]
 
         def product(dst, w_codes, w_scales, codes, scales):
             nc.tensor.matmul_mx(
@@ -191,26 +190,32 @@ def tile_picked_sub_mlp_relu_sub_e_kernel(tc, xT, w1, w2, gate, offs, pos1, pos2
         relu(True, first(2, 1, left), 1, left)
         quantize_h(0, whole)
         relu(True, first(3, 1, right), 1, right)
+        quantize_h(1, left)
         relu(False, first(4, 2, left), 2, left)
         relu(True, first(5, 2, right), 2, right)
-        quantize_h(1, whole)
+        quantize_h(1, right)
         quantize_h(2, left)
-        y_early = [bank(6, [SLICE]), bank(7, [SLICE + P]), bank(0, [2 * SLICE])]
-        second(y_early[0][:], 0, 0, whole)
-        second(y_early[1][:, 0:SLICE], 0, 1, whole)
-        second(y_early[1][:, SLICE:], 0, 2, left)
-        second(y_early[2][:, 0:SLICE], 1, 0, whole)
-        second(y_early[2][:, SLICE:], 1, 1, whole)
-        nc.vector.tensor_copy(y[0][:, 0:SLICE], y_early[0][:])
         quantize_h(2, right)
-        y_late = [bank(1, [P]), bank(2, [SLICE])]
-        second(y_late[1][:, left], 1, 2, left)
-        second(y_late[0][:], 0, 2, right)
-        second(y_late[1][:, right], 1, 2, right)
-        nc.vector.tensor_copy(y[0][:, SLICE : S - P], y_early[1][:])
-        nc.scalar.copy(y[1][:, 0 : 2 * SLICE], y_early[2][:])
-        nc.vector.tensor_copy(y[0][:, S - P : S], y_late[0][:])
-        nc.scalar.copy(y[1][:, 2 * SLICE : S], y_late[1][:])
+
+        y = [sb([P, S], F32, name) for name in ("h_woven2", "y1")]
+
+        def leave(engine, number, b, parts):
+            width = sum(cols.stop - cols.start for s, cols in parts)
+            sums = bank(number, [width])
+            at = 0
+            for s, cols in parts:
+                second(sums[:, at : at + cols.stop - cols.start], b, s, cols)
+                at = at + cols.stop - cols.start
+            start = parts[0][0] * SLICE + parts[0][1].start
+            engine(y[b][:, start : start + width], sums[:])
+
+        leave(nc.scalar.copy, 6, 1, [(0, whole)])
+        leave(nc.vector.tensor_copy, 7, 0, [(0, whole)])
+        leave(nc.scalar.copy, 0, 0, [(1, whole)])
+        leave(nc.vector.tensor_copy, 2, 0, [(2, left)])
+        leave(nc.vector.tensor_copy, 3, 0, [(2, right)])
+        leave(nc.scalar.copy, 1, 1, [(1, whole), (2, left)])
+        leave(nc.scalar.copy, 5, 1, [(2, right)])
 
         pieces = [slice(c * P, (c + 1) * P) for c in range(PIECES)]
         gated = [sb([P, V], F32, f"gated{d}") for d in range(D)]
@@ -231,7 +236,7 @@ def tile_picked_sub_mlp_relu_sub_e_kernel(tc, xT, w1, w2, gate, offs, pos1, pos2
             nc.sync.dma_start(out=out[b * P : (b + 1) * P, cols], in_=result[b][:, cols])
 
         sums0 = bank(4, [V])
-        turned = [bank(5 + d, [V]) for d in range(PLAIN)]
+        turned = [bank(number, [V]) for number in (6, 7, 5)]
         for d in range(2):
             fetch_gated(gated[d], 0, d)
             for c in range(PIECES):

@@ -75,7 +75,7 @@ def tile_picked_sub_mlp_relu_sub_e_kernel(tc, xT, w1, w2, gate, offs, pos1, pos2
         x_codes = []
         x_scales = [sb([P, SLICE], U8, f"x_scales{s}") for s in range(3)]
         flat = sb([P, 3, S], BF16, "flat")
-        flat_last = [None] + [sb([P, SLICE], BF16, f"flat_last{s}") for s in (1, 2)]
+        flat_last = [None, sb([P, SLICE], BF16, "flat_last1"), sb([P, P], BF16, "flat_last2")]
 
         def gather_flat(dst, j, cols):
             nc.scalar.activation(dst, x_raw[j][:].indirect(places(offs_sb, cols)), COPY)
@@ -120,10 +120,10 @@ def tile_picked_sub_mlp_relu_sub_e_kernel(tc, xT, w1, w2, gate, offs, pos1, pos2
             )
 
         gather_into(x_woven[0][:, :, 3], 3, slices[0])
-        for s in (1, 2):
-            gather_flat(flat_last[s][:], 3, slices[s])
+        gather_flat(flat_last[1][:], 3, slices[1])
+        gather_flat(flat_last[2][:], 3, slice(2 * SLICE, S - P))
         nc.vector.tensor_copy(x_woven[1][:, :, 3], flat_last[1][:])
-        nc.vector.tensor_copy(x_woven[2][:, :, 3], flat_last[2][:])
+        nc.vector.tensor_copy(x_woven[2][:, 0:P, 3], flat_last[2][:])
         x_codes.append(sb([P, SLICE], U32, "flat_last2"))
         quantize(x_codes[0][:], x_scales[0][:], x_woven[0][:])
         weave_w1(nc.scalar.copy, 0, slice(0, 32))
@@ -131,9 +131,12 @@ def tile_picked_sub_mlp_relu_sub_e_kernel(tc, xT, w1, w2, gate, offs, pos1, pos2
         weave_w1(nc.vector.tensor_copy, 2, slice(0, 32))
         weave_w1(nc.vector.tensor_copy, 3, slice(12, 32))
         weave_w1(nc.scalar.copy, 3, slice(0, 12))
+        flat_end = reused.tile([P, P], BF16, name="flat_end", offset=1024, align_bytes=64)
+        gather_flat(flat_end[:], 3, slice(S - P, S))
         for t in range(PACK):
             tile_t = slice(t * P, (t + 1) * P)
             quantize(w1_codes[:, tile_t], w1_scales[:, tile_t], w1_woven[:, t])
+        nc.vector.tensor_copy(x_woven[2][:, P:SLICE, 3], flat_end[:])
         for s in (1, 2):
             x_codes.append(reused.tile([P, SLICE], U32, name=f"x_codes{s}", offset=(s - 1) * 1024, align_bytes=64))
             quantize(x_codes[s][:], x_scales[s][:], x_woven[s][:])
@@ -261,7 +264,8 @@ def tile_picked_sub_mlp_relu_sub_e_kernel(tc, xT, w1, w2, gate, offs, pos1, pos2
         back0 = bank(0, [V])
         for c in range(PIECES):
             flip(back0[:, pieces[c]], summed[:, pieces[c]], True, True)
-        finish(0, back0[:], pair, slice(0, V))
+        for cols in (pieces[0], slice(P, V)):
+            finish(0, back0[:, cols], pair, cols)
         for c in range(PIECES):
             for d in range(1, PLAIN):
                 scale(d, c)

@@ -22,6 +22,7 @@ SLICE = 256
 LANE = 16
 PIECES = V // P
 PLAIN = 3
+VECTOR_SHARE = (80, 56)
 
 
 def tile_picked_sub_mlp_relu_sub_e_kernel(tc, xT, w1, w2, gate, offs, pos1, pos2, pos3, pos4, out):
@@ -43,9 +44,8 @@ def tile_picked_sub_mlp_relu_sub_e_kernel(tc, xT, w1, w2, gate, offs, pos1, pos2
         offs_sb = keep.tile([P, S // LANE], U16, name="offs_sb")
         pos_sb = [keep.tile([P, V // LANE], U16, name=f"pos_sb{d}") for d in range(D)]
         x_raw = [sb([P, T], F32, f"x_raw{j}") for j in range(PACK)]
-        w1_raw = [sb([P, PACK, P], F32, f"w1_raw{q}") for q in range(PACK - 1)]
-        w1_raw.append(reused.tile([P, PACK, P], F32, name="w1_last", offset=0, align_bytes=64))
-        w2_raw = [sb([P, PACK, P], F32, f"w2_raw{b}") for b in range(2)]
+        w1_raw = reused.tile([P, PACK, H], F32, name="w1_raw", offset=0, align_bytes=64)
+        w2_raw = sb([P, PACK, N], F32, "w2_raw")
         gates = sb([P, D, V], F32, "gates")
         gate_cols = sb([P, PLAIN, PIECES], F32, "gate_cols")
 
@@ -56,10 +56,8 @@ def tile_picked_sub_mlp_relu_sub_e_kernel(tc, xT, w1, w2, gate, offs, pos1, pos2
         nc.sync.dma_start(offs_sb[:], offs)
         for j in range(1, PACK):
             nc.sync.dma_start(out=x_raw[j][:], in_=xv[:, j, :])
-        for q in range(PACK):
-            nc.sync.dma_start(out=w1_raw[q][:], in_=w1v[:, :, q * P : (q + 1) * P])
-        for b in range(2):
-            nc.sync.dma_start(out=w2_raw[b][:], in_=w2v[:, :, b * P : (b + 1) * P])
+        nc.sync.dma_start(out=w1_raw[:], in_=w1v)
+        nc.sync.dma_start(out=w2_raw[:], in_=w2v)
         nc.sync.dma_start(out=gates[:], in_=gate[:, 0:P, :].rearrange("d p v -> p d v"))
         for d, p in enumerate((pos1, pos2, pos3, pos4)):
             nc.sync.dma_start(pos_sb[d][:], p)
@@ -75,7 +73,7 @@ def tile_picked_sub_mlp_relu_sub_e_kernel(tc, xT, w1, w2, gate, offs, pos1, pos2
         x_codes = []
         x_scales = [sb([P, SLICE], U8, f"x_scales{s}") for s in range(3)]
         flat = sb([P, 3, S], BF16, "flat")
-        flat_last = [None, sb([P, SLICE], BF16, "flat_last1"), sb([P, P], BF16, "flat_last2")]
+        flat_last = [None, sb([P, SLICE], BF16, "flat_last1"), sb([P, SLICE], BF16, "flat_last2")]
 
         def gather_flat(dst, j, cols):
             nc.scalar.activation(dst, x_raw[j][:].indirect(places(offs_sb, cols)), COPY)
@@ -103,10 +101,11 @@ def tile_picked_sub_mlp_relu_sub_e_kernel(tc, xT, w1, w2, gate, offs, pos1, pos2
         w1_codes = sb([P, H], U32, "w1_codes")
         w1_scales = sb([P, H], U8, "w1_scales")
 
-        def weave_w1(engine, q, m):
+        def weave_w1(engine, pair, m):
+            two = slice(2 * pair, 2 * pair + 2)
             engine(
-                w1_woven[:, :, 32 * q + m.start : 32 * q + m.stop].rearrange("p t m j -> p m j t"),
-                w1_raw[q][:, :, PACK * m.start : PACK * m.stop].rearrange("p j (m t) -> p m j t", t=PACK),
+                w1_woven[:, two, m, :].rearrange("p t m j -> p m j t"),
+                w1_raw[:].rearrange("p j (m t) -> p m j t", t=PACK)[:, m, :, two],
             )
 
         w2_woven = [sb([P, P, PACK], BF16, f"w2_woven{b}") for b in range(2)]
@@ -116,30 +115,24 @@ def tile_picked_sub_mlp_relu_sub_e_kernel(tc, xT, w1, w2, gate, offs, pos1, pos2
         def weave_w2(engine, b):
             engine(
                 w2_woven[b][:].rearrange("p (c i) j -> p c j i", i=4),
-                w2_raw[b][:].rearrange("p j (c i) -> p c j i", i=4),
+                w2_raw[:, :, b * P : (b + 1) * P].rearrange("p j (c i) -> p c j i", i=4),
             )
 
         gather_into(x_woven[0][:, :, 3], 3, slices[0])
-        gather_flat(flat_last[1][:], 3, slices[1])
-        gather_flat(flat_last[2][:], 3, slice(2 * SLICE, S - P))
-        nc.vector.tensor_copy(x_woven[1][:, :, 3], flat_last[1][:])
-        nc.vector.tensor_copy(x_woven[2][:, 0:P, 3], flat_last[2][:])
-        x_codes.append(sb([P, SLICE], U32, "flat_last2"))
-        quantize(x_codes[0][:], x_scales[0][:], x_woven[0][:])
-        weave_w1(nc.scalar.copy, 0, slice(0, 32))
-        weave_w1(nc.scalar.copy, 1, slice(0, 32))
-        weave_w1(nc.vector.tensor_copy, 2, slice(0, 32))
-        weave_w1(nc.vector.tensor_copy, 3, slice(12, 32))
-        weave_w1(nc.scalar.copy, 3, slice(0, 12))
-        flat_end = reused.tile([P, P], BF16, name="flat_end", offset=1024, align_bytes=64)
-        gather_flat(flat_end[:], 3, slice(S - P, S))
+        for s in (1, 2):
+            gather_flat(flat_last[s][:], 3, slices[s])
+        x_codes.extend(sb([P, SLICE], U32, f"x_codes{s}") for s in range(2))
+        x_codes.append(reused.tile([P, SLICE], U32, name="x_codes2", offset=0, align_bytes=64))
+        for s in (1, 2):
+            nc.vector.tensor_copy(x_woven[s][:, :, 3], flat_last[s][:])
+            quantize(x_codes[s - 1][:], x_scales[s - 1][:], x_woven[s - 1][:])
+        for pair, share in enumerate(VECTOR_SHARE):
+            weave_w1(nc.vector.tensor_copy, pair, slice(0, share))
+            weave_w1(nc.scalar.copy, pair, slice(share, P))
         for t in range(PACK):
             tile_t = slice(t * P, (t + 1) * P)
             quantize(w1_codes[:, tile_t], w1_scales[:, tile_t], w1_woven[:, t])
-        nc.vector.tensor_copy(x_woven[2][:, P:SLICE, 3], flat_end[:])
-        for s in (1, 2):
-            x_codes.append(reused.tile([P, SLICE], U32, name=f"x_codes{s}", offset=(s - 1) * 1024, align_bytes=64))
-            quantize(x_codes[s][:], x_scales[s][:], x_woven[s][:])
+        quantize(x_codes[2][:], x_scales[2][:], x_woven[2][:])
         for b in range(2):
             weave_w2(nc.scalar.copy, b)
             quantize(w2_codes[b][:], w2_scales[b][:], w2_woven[b][:])
@@ -159,11 +152,14 @@ def tile_picked_sub_mlp_relu_sub_e_kernel(tc, xT, w1, w2, gate, offs, pos1, pos2
                 stop=True,
             )
 
-        def first(number, s, cols):
-            sums = bank(number, [PACK, cols.stop - cols.start])
-            for t in range(PACK):
+        def first_tiles(sums, s, cols, tiles):
+            for t in tiles:
                 tile_t = slice(t * P, (t + 1) * P)
                 product(sums[:, t, :], w1_codes[:, tile_t], w1_scales[:, tile_t], x_codes[s][:, cols], x_scales[s][:, cols])
+
+        def first(number, s, cols):
+            sums = bank(number, [PACK, P])
+            first_tiles(sums, s, cols, range(PACK))
             return sums
 
         def relu(on_scalar, sums, s, cols):
@@ -185,11 +181,15 @@ def tile_picked_sub_mlp_relu_sub_e_kernel(tc, xT, w1, w2, gate, offs, pos1, pos2
         unread = bank(7, [2 * SLICE])
         at = 0
         for width in (256, 128, 64):
-            product(unread[:, at : at + width], x_codes[0][:, left], x_scales[0][:, left], x_codes[0][:, 0:width], x_scales[0][:, 0:width])
+            product(unread[:, at : at + width], x_codes[1][:, left], x_scales[1][:, left], x_codes[1][:, 0:width], x_scales[1][:, 0:width])
             at = at + width
 
-        relu(True, first(0, 0, left), 0, left)
-        relu(False, first(1, 0, right), 0, right)
+        opening = [(bank(0, [PACK, P]), left), (bank(1, [PACK, P]), right)]
+        for tiles in ((0, 1), (2, 3)):
+            for sums, cols in opening:
+                first_tiles(sums, 0, cols, tiles)
+        relu(True, opening[0][0], 0, left)
+        relu(False, opening[1][0], 0, right)
         relu(True, first(2, 1, left), 1, left)
         quantize_h(0, whole)
         relu(True, first(3, 1, right), 1, right)

@@ -22,7 +22,8 @@ SLICE = 256
 LANE = 16
 PIECES = V // P
 PLAIN = 3
-VECTOR_SHARE = (80, 56)
+FIRST_SHARE = 10
+VECTOR_SHARE = (42, 36)
 
 
 def tile_picked_sub_mlp_relu_sub_e_kernel(tc, xT, w1, w2, gate, offs, pos1, pos2, pos3, pos4, out):
@@ -44,8 +45,8 @@ def tile_picked_sub_mlp_relu_sub_e_kernel(tc, xT, w1, w2, gate, offs, pos1, pos2
         offs_sb = keep.tile([P, S // LANE], U16, name="offs_sb")
         pos_sb = [keep.tile([P, V // LANE], U16, name=f"pos_sb{d}") for d in range(D)]
         x_raw = [sb([P, T], F32, f"x_raw{j}") for j in range(PACK)]
-        w1_raw = reused.tile([P, PACK, H], F32, name="w1_raw", offset=0, align_bytes=64)
-        w2_raw = sb([P, PACK, N], F32, "w2_raw")
+        w1_raw = [sb([P, PACK, H // 2], F32, "w1_raw0"), reused.tile([P, PACK, H // 2], F32, name="w1_raw1", offset=0, align_bytes=64)]
+        w2_raw = [sb([P, PACK, P], F32, f"w2_raw{b}") for b in range(2)]
         gates = sb([P, D, V], F32, "gates")
         gate_cols = sb([P, PLAIN, PIECES], F32, "gate_cols")
 
@@ -56,8 +57,10 @@ def tile_picked_sub_mlp_relu_sub_e_kernel(tc, xT, w1, w2, gate, offs, pos1, pos2
         nc.sync.dma_start(offs_sb[:], offs)
         for j in range(1, PACK):
             nc.sync.dma_start(out=x_raw[j][:], in_=xv[:, j, :])
-        nc.sync.dma_start(out=w1_raw[:], in_=w1v)
-        nc.sync.dma_start(out=w2_raw[:], in_=w2v)
+        for half in range(2):
+            nc.sync.dma_start(out=w1_raw[half][:], in_=w1v[:, :, half * H // 2 : (half + 1) * H // 2])
+        for b in range(2):
+            nc.sync.dma_start(out=w2_raw[b][:], in_=w2v[:, :, b * P : (b + 1) * P])
         nc.sync.dma_start(out=gates[:], in_=gate[:, 0:P, :].rearrange("d p v -> p d v"))
         for d, p in enumerate((pos1, pos2, pos3, pos4)):
             nc.sync.dma_start(pos_sb[d][:], p)
@@ -73,7 +76,7 @@ def tile_picked_sub_mlp_relu_sub_e_kernel(tc, xT, w1, w2, gate, offs, pos1, pos2
         x_codes = []
         x_scales = [sb([P, SLICE], U8, f"x_scales{s}") for s in range(3)]
         flat = sb([P, 3, S], BF16, "flat")
-        flat_last = [None, sb([P, SLICE], BF16, "flat_last1"), sb([P, SLICE], BF16, "flat_last2")]
+        flat_last = [None, sb([P, SLICE], BF16, "flat_last1"), sb([P, P], BF16, "flat_last2")]
 
         def gather_flat(dst, j, cols):
             nc.scalar.activation(dst, x_raw[j][:].indirect(places(offs_sb, cols)), COPY)
@@ -101,11 +104,10 @@ def tile_picked_sub_mlp_relu_sub_e_kernel(tc, xT, w1, w2, gate, offs, pos1, pos2
         w1_codes = sb([P, H], U32, "w1_codes")
         w1_scales = sb([P, H], U8, "w1_scales")
 
-        def weave_w1(engine, pair, m):
-            two = slice(2 * pair, 2 * pair + 2)
+        def weave_w1(engine, half, tiles, m):
             engine(
-                w1_woven[:, two, m, :].rearrange("p t m j -> p m j t"),
-                w1_raw[:].rearrange("p j (m t) -> p m j t", t=PACK)[:, m, :, two],
+                w1_woven[:, tiles, 64 * half + m.start : 64 * half + m.stop, :].rearrange("p t m j -> p m j t"),
+                w1_raw[half][:].rearrange("p j (m t) -> p m j t", t=PACK)[:, m, :, tiles],
             )
 
         w2_woven = [sb([P, P, PACK], BF16, f"w2_woven{b}") for b in range(2)]
@@ -115,23 +117,29 @@ def tile_picked_sub_mlp_relu_sub_e_kernel(tc, xT, w1, w2, gate, offs, pos1, pos2
         def weave_w2(engine, b):
             engine(
                 w2_woven[b][:].rearrange("p (c i) j -> p c j i", i=4),
-                w2_raw[:, :, b * P : (b + 1) * P].rearrange("p j (c i) -> p c j i", i=4),
+                w2_raw[b][:].rearrange("p j (c i) -> p c j i", i=4),
             )
 
         gather_into(x_woven[0][:, :, 3], 3, slices[0])
-        for s in (1, 2):
-            gather_flat(flat_last[s][:], 3, slices[s])
-        x_codes.extend(sb([P, SLICE], U32, f"x_codes{s}") for s in range(2))
-        x_codes.append(reused.tile([P, SLICE], U32, name="x_codes2", offset=0, align_bytes=64))
-        for s in (1, 2):
-            nc.vector.tensor_copy(x_woven[s][:, :, 3], flat_last[s][:])
-            quantize(x_codes[s - 1][:], x_scales[s - 1][:], x_woven[s - 1][:])
+        gather_flat(flat_last[1][:], 3, slices[1])
+        gather_flat(flat_last[2][:], 3, slice(2 * SLICE, S - P))
+        x_codes.extend(sb([P, SLICE], U32, f"x_codes{s}") for s in range(3))
+        nc.vector.tensor_copy(x_woven[1][:, :, 3], flat_last[1][:])
+        nc.vector.tensor_copy(x_woven[2][:, 0:P, 3], flat_last[2][:])
+        weave_w1(nc.vector.tensor_copy, 0, slice(0, PACK), slice(0, FIRST_SHARE))
+        weave_w1(nc.scalar.copy, 0, slice(0, PACK), slice(FIRST_SHARE, 64))
+        for s in range(2):
+            quantize(x_codes[s][:], x_scales[s][:], x_woven[s][:])
         for pair, share in enumerate(VECTOR_SHARE):
-            weave_w1(nc.vector.tensor_copy, pair, slice(0, share))
-            weave_w1(nc.scalar.copy, pair, slice(share, P))
+            two = slice(2 * pair, 2 * pair + 2)
+            weave_w1(nc.vector.tensor_copy, 1, two, slice(0, share))
+            weave_w1(nc.scalar.copy, 1, two, slice(share, 64))
+        flat_end = reused.tile([P, P], BF16, name="flat_end", offset=0, align_bytes=64)
+        gather_flat(flat_end[:], 3, slice(S - P, S))
         for t in range(PACK):
             tile_t = slice(t * P, (t + 1) * P)
             quantize(w1_codes[:, tile_t], w1_scales[:, tile_t], w1_woven[:, t])
+        nc.vector.tensor_copy(x_woven[2][:, P:SLICE, 3], flat_end[:])
         quantize(x_codes[2][:], x_scales[2][:], x_woven[2][:])
         for b in range(2):
             weave_w2(nc.scalar.copy, b)
@@ -184,12 +192,8 @@ def tile_picked_sub_mlp_relu_sub_e_kernel(tc, xT, w1, w2, gate, offs, pos1, pos2
             product(unread[:, at : at + width], x_codes[1][:, left], x_scales[1][:, left], x_codes[1][:, 0:width], x_scales[1][:, 0:width])
             at = at + width
 
-        opening = [(bank(0, [PACK, P]), left), (bank(1, [PACK, P]), right)]
-        for tiles in ((0, 1), (2, 3)):
-            for sums, cols in opening:
-                first_tiles(sums, 0, cols, tiles)
-        relu(True, opening[0][0], 0, left)
-        relu(False, opening[1][0], 0, right)
+        relu(True, first(0, 0, left), 0, left)
+        relu(False, first(1, 0, right), 0, right)
         relu(True, first(2, 1, left), 1, left)
         quantize_h(0, whole)
         relu(True, first(3, 1, right), 1, right)
@@ -262,14 +266,15 @@ def tile_picked_sub_mlp_relu_sub_e_kernel(tc, xT, w1, w2, gate, offs, pos1, pos2
         for c in range(PIECES):
             scale(0, c)
         back0 = bank(0, [V])
+        back1 = [bank(1 + c, [P]) for c in range(PIECES)]
         for c in range(PIECES):
             flip(back0[:, pieces[c]], summed[:, pieces[c]], True, True)
+        for c in range(PIECES):
+            flip(back1[c][:], scaled[0][:, pieces[c]], True, False)
         for cols in (pieces[0], slice(P, V)):
             finish(0, back0[:, cols], pair, cols)
         for c in range(PIECES):
             for d in range(1, PLAIN):
                 scale(d, c)
-            back1 = bank(1 + c, [P])
-            for d in range(PLAIN):
-                flip(back1[:], scaled[d][:, pieces[c]], d == 0, d == PLAIN - 1)
-            finish(1, back1[:], gated_last, pieces[c])
+                flip(back1[c][:], scaled[d][:, pieces[c]], False, d == PLAIN - 1)
+            finish(1, back1[c][:], gated_last, pieces[c])

@@ -22,8 +22,8 @@ SLICE = 256
 LANE = 16
 PIECES = V // P
 PLAIN = 3
-FIRST_SHARE = 10
-VECTOR_SHARE = (42, 36)
+FIRST_SHARE = 22
+VECTOR_SHARE = (30, 48)
 
 
 def tile_picked_sub_mlp_relu_sub_e_kernel(tc, xT, w1, w2, gate, offs, pos1, pos2, pos3, pos4, out):
@@ -76,7 +76,7 @@ def tile_picked_sub_mlp_relu_sub_e_kernel(tc, xT, w1, w2, gate, offs, pos1, pos2
         x_codes = []
         x_scales = [sb([P, SLICE], U8, f"x_scales{s}") for s in range(3)]
         flat = sb([P, 3, S], BF16, "flat")
-        flat_last = [None, sb([P, SLICE], BF16, "flat_last1"), sb([P, P], BF16, "flat_last2")]
+        flat_last = [None, sb([P, SLICE], BF16, "flat_last1"), sb([P, SLICE], BF16, "flat_last2")]
 
         def gather_flat(dst, j, cols):
             nc.scalar.activation(dst, x_raw[j][:].indirect(places(offs_sb, cols)), COPY)
@@ -121,26 +121,25 @@ def tile_picked_sub_mlp_relu_sub_e_kernel(tc, xT, w1, w2, gate, offs, pos1, pos2
             )
 
         gather_into(x_woven[0][:, :, 3], 3, slices[0])
-        gather_flat(flat_last[1][:], 3, slices[1])
-        gather_flat(flat_last[2][:], 3, slice(2 * SLICE, S - P))
-        x_codes.extend(sb([P, SLICE], U32, f"x_codes{s}") for s in range(3))
-        nc.vector.tensor_copy(x_woven[1][:, :, 3], flat_last[1][:])
-        nc.vector.tensor_copy(x_woven[2][:, 0:P, 3], flat_last[2][:])
+        x_codes.append(sb([P, SLICE], U32, "x_codes0"))
+        for at in (0, P):
+            gather_flat(flat_last[1][:, at : at + P], 3, slice(SLICE + at, SLICE + at + P))
+            nc.vector.tensor_copy(x_woven[1][:, at : at + P, 3], flat_last[1][:, at : at + P])
+            quantize(x_codes[0][:, at : at + P], x_scales[0][:, at : at + P], x_woven[0][:, at : at + P])
+        gather_flat(flat_last[2][:], 3, slices[2])
+        nc.vector.tensor_copy(x_woven[2][:, :, 3], flat_last[2][:])
         weave_w1(nc.vector.tensor_copy, 0, slice(0, PACK), slice(0, FIRST_SHARE))
         weave_w1(nc.scalar.copy, 0, slice(0, PACK), slice(FIRST_SHARE, 64))
-        for s in range(2):
-            quantize(x_codes[s][:], x_scales[s][:], x_woven[s][:])
         for pair, share in enumerate(VECTOR_SHARE):
             two = slice(2 * pair, 2 * pair + 2)
             weave_w1(nc.vector.tensor_copy, 1, two, slice(0, share))
             weave_w1(nc.scalar.copy, 1, two, slice(share, 64))
-        flat_end = reused.tile([P, P], BF16, name="flat_end", offset=0, align_bytes=64)
-        gather_flat(flat_end[:], 3, slice(S - P, S))
         for t in range(PACK):
             tile_t = slice(t * P, (t + 1) * P)
             quantize(w1_codes[:, tile_t], w1_scales[:, tile_t], w1_woven[:, t])
-        nc.vector.tensor_copy(x_woven[2][:, P:SLICE, 3], flat_end[:])
-        quantize(x_codes[2][:], x_scales[2][:], x_woven[2][:])
+        for s in (1, 2):
+            x_codes.append(reused.tile([P, SLICE], U32, name=f"x_codes{s}", offset=(s - 1) * 1024, align_bytes=64))
+            quantize(x_codes[s][:], x_scales[s][:], x_woven[s][:])
         for b in range(2):
             weave_w2(nc.scalar.copy, b)
             quantize(w2_codes[b][:], w2_scales[b][:], w2_woven[b][:])
@@ -189,7 +188,7 @@ def tile_picked_sub_mlp_relu_sub_e_kernel(tc, xT, w1, w2, gate, offs, pos1, pos2
         unread = bank(7, [2 * SLICE])
         at = 0
         for width in (256, 128, 64):
-            product(unread[:, at : at + width], x_codes[1][:, left], x_scales[1][:, left], x_codes[1][:, 0:width], x_scales[1][:, 0:width])
+            product(unread[:, at : at + width], x_codes[0][:, left], x_scales[0][:, left], x_codes[0][:, 0:width], x_scales[0][:, 0:width])
             at = at + width
 
         relu(True, first(0, 0, left), 0, left)
@@ -204,7 +203,7 @@ def tile_picked_sub_mlp_relu_sub_e_kernel(tc, xT, w1, w2, gate, offs, pos1, pos2
         quantize_h(2, left)
         quantize_h(2, right)
 
-        y = [sb([P, S], F32, name) for name in ("h_woven2", "y1")]
+        y = [sb([P, S], F32, name) for name in ("y0", "h_woven2")]
 
         def leave(engine, number, b, parts):
             width = sum(cols.stop - cols.start for s, cols in parts)
@@ -216,13 +215,12 @@ def tile_picked_sub_mlp_relu_sub_e_kernel(tc, xT, w1, w2, gate, offs, pos1, pos2
             start = parts[0][0] * SLICE + parts[0][1].start
             engine(y[b][:, start : start + width], sums[:])
 
-        leave(nc.scalar.copy, 6, 1, [(0, whole)])
-        leave(nc.vector.tensor_copy, 7, 0, [(0, whole)])
+        leave(nc.scalar.copy, 6, 0, [(0, whole)])
         leave(nc.scalar.copy, 0, 0, [(1, whole)])
-        leave(nc.vector.tensor_copy, 2, 0, [(2, left)])
-        leave(nc.vector.tensor_copy, 3, 0, [(2, right)])
-        leave(nc.scalar.copy, 1, 1, [(1, whole), (2, left)])
-        leave(nc.scalar.copy, 5, 1, [(2, right)])
+        leave(nc.vector.tensor_copy, 7, 1, [(0, whole), (1, whole)])
+        leave(nc.scalar.copy, 2, 0, [(2, left)])
+        leave(nc.scalar.copy, 3, 0, [(2, right)])
+        leave(nc.scalar.copy, 5, 1, [(2, whole)])
 
         pieces = [slice(c * P, (c + 1) * P) for c in range(PIECES)]
         gated = [sb([P, V], F32, f"gated{d}") for d in range(D)]

@@ -125,10 +125,11 @@ def tile_picked_sub_mlp_relu_sub_e_kernel(tc, xT, w1, w2, gate, offs, pos1, pos2
         for at in (0, P):
             gather_flat(flat_last[1][:, at : at + P], 3, slice(SLICE + at, SLICE + at + P))
             nc.vector.tensor_copy(x_woven[1][:, at : at + P, 3], flat_last[1][:, at : at + P])
+            if at == P:
+                weave_w1(nc.vector.tensor_copy, 0, slice(0, PACK), slice(0, FIRST_SHARE))
             quantize(x_codes[0][:, at : at + P], x_scales[0][:, at : at + P], x_woven[0][:, at : at + P])
         gather_flat(flat_last[2][:], 3, slices[2])
         nc.vector.tensor_copy(x_woven[2][:, :, 3], flat_last[2][:])
-        weave_w1(nc.vector.tensor_copy, 0, slice(0, PACK), slice(0, FIRST_SHARE))
         weave_w1(nc.scalar.copy, 0, slice(0, PACK), slice(FIRST_SHARE, 64))
         for pair, share in enumerate(VECTOR_SHARE):
             two = slice(2 * pair, 2 * pair + 2)
@@ -194,7 +195,8 @@ def tile_picked_sub_mlp_relu_sub_e_kernel(tc, xT, w1, w2, gate, offs, pos1, pos2
         relu(True, first(0, 0, left), 0, left)
         relu(False, first(1, 0, right), 0, right)
         relu(True, first(2, 1, left), 1, left)
-        quantize_h(0, whole)
+        quantize_h(0, left)
+        quantize_h(0, right)
         relu(True, first(3, 1, right), 1, right)
         quantize_h(1, left)
         relu(False, first(4, 2, left), 2, left)

@@ -186,12 +186,6 @@ def tile_picked_sub_mlp_relu_sub_e_kernel(tc, xT, w1, w2, gate, offs, pos1, pos2
 
         whole, left, right = slice(0, SLICE), slice(0, P), slice(P, SLICE)
 
-        unread = bank(7, [2 * SLICE])
-        at = 0
-        for width in (256, 128, 64):
-            product(unread[:, at : at + width], x_codes[0][:, left], x_scales[0][:, left], x_codes[0][:, 0:width], x_scales[0][:, 0:width])
-            at = at + width
-
         relu(True, first(0, 0, left), 0, left)
         relu(False, first(1, 0, right), 0, right)
         relu(True, first(2, 1, left), 1, left)

from contextlib import ExitStack

import concourse.mybir as mybir
from concourse.masks import make_identity

K, T, D, S, V, H, N = 512, 2048, 4, 768, 384, 512, 256
FLOPS = 2 * S * (K * H + H * N)

F32 = mybir.dt.float32
BF16 = mybir.dt.bfloat16
U32 = mybir.dt.uint32
U16 = mybir.dt.uint16
U8 = mybir.dt.uint8
FP8X4 = mybir.dt.float8_e4m3fn_x4
ADD, MULT = mybir.AluOpType.add, mybir.AluOpType.mult
RELU = mybir.ActivationFunctionType.Relu
COPY = mybir.ActivationFunctionType.Copy

P = 128
PACK = 4
SLICE = 256
LANE = 16
PIECES = V // P
PLAIN = 3
FIRST_SHARE = 22
VECTOR_SHARE = (30, 48)


def tile_picked_sub_mlp_relu_sub_e_kernel(tc, xT, w1, w2, gate, offs, pos1, pos2, pos3, pos4, out):
    nc = tc.nc
    with ExitStack() as ctx:
        keep = ctx.enter_context(tc.tile_pool(name="keep", bufs=1))
        reused = ctx.enter_context(tc.tile_pool(name="reused", bufs=1))
        psum = ctx.enter_context(tc.psum_pool(name="psum", bufs=1))

        def sb(shape, dtype, name):
            return keep.tile(shape, dtype, name=name, align_bytes=64)

        def bank(number, shape):
            return psum.tile([P] + shape, F32, name=f"bank{number}")

        def places(lists, cols):
            return lists[:, cols.start // LANE : cols.stop // LANE]

        offs_sb = keep.tile([P, S // LANE], U16, name="offs_sb")
        pos_sb = [keep.tile([P, V // LANE], U16, name=f"pos_sb{d}") for d in range(D)]
        x_raw = [sb([P, T], F32, f"x_raw{j}") for j in range(PACK)]
        w1_raw = [sb([P, PACK, H // 2], F32, "w1_raw0"), reused.tile([P, PACK, H // 2], F32, name="w1_raw1", offset=0, align_bytes=64)]
        w2_raw = [sb([P, PACK, P], F32, f"w2_raw{b}") for b in range(2)]
        gates = sb([P, D, V], F32, "gates")
        gate_cols = sb([P, PLAIN, PIECES], F32, "gate_cols")

        xv = xT.rearrange("(p j) t -> p j t", j=PACK)
        w1v = w1.rearrange("(p j) c -> p j c", j=PACK)
        w2v = w2.rearrange("(p j) c -> p j c", j=PACK)
        nc.sync.dma_start(out=x_raw[0][:], in_=xv[:, 0, :])
        nc.sync.dma_start(offs_sb[:], offs)
        for j in range(1, PACK):
            nc.sync.dma_start(out=x_raw[j][:], in_=xv[:, j, :])
        for half in range(2):
            nc.sync.dma_start(out=w1_raw[half][:], in_=w1v[:, :, half * H // 2 : (half + 1) * H // 2])
        for b in range(2):
            nc.sync.dma_start(out=w2_raw[b][:], in_=w2v[:, :, b * P : (b + 1) * P])
        nc.sync.dma_start(out=gates[:], in_=gate[:, 0:P, :].rearrange("d p v -> p d v"))
        for d, p in enumerate((pos1, pos2, pos3, pos4)):
            nc.sync.dma_start(pos_sb[d][:], p)
        thirds = gate.rearrange("d m v -> (d m v)").rearrange("(k r) -> k r", k=D * PIECES)
        with nc.allow_non_contiguous_dma(reason="one gate value a partition"):
            nc.sync.dma_start(out=gate_cols[:].rearrange("p d c -> p (d c)"), in_=thirds[0 : PLAIN * PIECES, 0:P].rearrange("k p -> p k"))

        identity = sb([P, P], F32, "identity")
        make_identity(nc, identity[:])

        slices = [slice(s * SLICE, (s + 1) * SLICE) for s in range(S // SLICE)]
        x_woven = [sb([P, SLICE, PACK], BF16, f"x_woven{s}") for s in range(3)]
        x_codes = []
        x_scales = [sb([P, SLICE], U8, f"x_scales{s}") for s in range(3)]
        flat = sb([P, 3, S], BF16, "flat")
        flat_last = [None, sb([P, SLICE], BF16, "flat_last1"), sb([P, SLICE], BF16, "flat_last2")]

        def gather_flat(dst, j, cols):
            nc.scalar.activation(dst, x_raw[j][:].indirect(places(offs_sb, cols)), COPY)

        def gather_into(dst, j, cols):
            nc.vector.tensor_copy(dst, x_raw[j][:].indirect(places(offs_sb, cols)))

        def place(engine, s, planes):
            engine(x_woven[s][:, :, 0:planes], flat[:, 0:planes, slices[s]].rearrange("p j n -> p n j"))

        def quantize(codes, scales, values):
            nc.vector.quantize_mx(out=codes.bitcast(FP8X4), scales=scales, in_=values.rearrange("p n j -> p (n j)"))

        rest = slice(SLICE, S)
        gather_into(flat[:, 0, :], 0, slice(0, S))
        gather_into(flat[:, 1, slices[0]], 1, slices[0])
        place(nc.scalar.copy, 0, 2)
        gather_into(flat[:, 1, rest], 1, rest)
        gather_into(x_woven[0][:, :, 2], 2, slices[0])
        for s in (1, 2):
            gather_flat(flat[:, 2, slices[s]], 2, slices[s])
            place(nc.vector.tensor_copy, s, 3)

        w1_woven = sb([P, PACK, P, PACK], BF16, "w1_woven")
        w1_codes = sb([P, H], U32, "w1_codes")
        w1_scales = sb([P, H], U8, "w1_scales")

        def weave_w1(engine, half, tiles, m):
            engine(
                w1_woven[:, tiles, 64 * half + m.start : 64 * half + m.stop, :].rearrange("p t m j -> p m j t"),
                w1_raw[half][:].rearrange("p j (m t) -> p m j t", t=PACK)[:, m, :, tiles],
            )

        w2_woven = [sb([P, P, PACK], BF16, f"w2_woven{b}") for b in range(2)]
        w2_codes = [sb([P, P], U32, f"w2_codes{b}") for b in range(2)]
        w2_scales = [sb([P, P], U8, f"w2_scales{b}") for b in range(2)]

        def weave_w2(engine, b):
            engine(
                w2_woven[b][:].rearrange("p (c i) j -> p c j i", i=4),
                w2_raw[b][:].rearrange("p j (c i) -> p c j i", i=4),
            )

        gather_into(x_woven[0][:, :, 3], 3, slices[0])
        x_codes.append(sb([P, SLICE], U32, "x_codes0"))
        for at in (0, P):
            gather_flat(flat_last[1][:, at : at + P], 3, slice(SLICE + at, SLICE + at + P))
            nc.vector.tensor_copy(x_woven[1][:, at : at + P, 3], flat_last[1][:, at : at + P])
            if at == P:
                weave_w1(nc.vector.tensor_copy, 0, slice(0, PACK), slice(0, FIRST_SHARE))
            quantize(x_codes[0][:, at : at + P], x_scales[0][:, at : at + P], x_woven[0][:, at : at + P])
        gather_flat(flat_last[2][:], 3, slices[2])
        nc.vector.tensor_copy(x_woven[2][:, :, 3], flat_last[2][:])
        weave_w1(nc.scalar.copy, 0, slice(0, PACK), slice(FIRST_SHARE, 64))
        for pair, share in enumerate(VECTOR_SHARE):
            two = slice(2 * pair, 2 * pair + 2)
            weave_w1(nc.vector.tensor_copy, 1, two, slice(0, share))
            weave_w1(nc.scalar.copy, 1, two, slice(share, 64))
        for t in range(PACK):
            tile_t = slice(t * P, (t + 1) * P)
            quantize(w1_codes[:, tile_t], w1_scales[:, tile_t], w1_woven[:, t])
        for s in (1, 2):
            x_codes.append(reused.tile([P, SLICE], U32, name=f"x_codes{s}", offset=(s - 1) * 1024, align_bytes=64))
            quantize(x_codes[s][:], x_scales[s][:], x_woven[s][:])
        for b in range(2):
            weave_w2(nc.scalar.copy, b)
            quantize(w2_codes[b][:], w2_scales[b][:], w2_woven[b][:])

        h_woven = [sb([P, SLICE, PACK], BF16, f"h_woven{s}") for s in range(3)]
        h_codes = [sb([P, SLICE], U32, f"h_codes{s}") for s in range(3)]
        h_scales = [sb([P, SLICE], U8, f"h_scales{s}") for s in range(3)]

        def product(dst, w_codes, w_scales, codes, scales):
            nc.tensor.matmul_mx(
                out=dst,
                lhsT=w_codes.bitcast(FP8X4),
                lhsT_scale=w_scales,
                rhs=codes.bitcast(FP8X4),
                rhs_scale=scales,
                start=True,
                stop=True,
            )

        def first_tiles(sums, s, cols, tiles):
            for t in tiles:
                tile_t = slice(t * P, (t + 1) * P)
                product(sums[:, t, :], w1_codes[:, tile_t], w1_scales[:, tile_t], x_codes[s][:, cols], x_scales[s][:, cols])

        def first(number, s, cols):
            sums = bank(number, [PACK, P])
            first_tiles(sums, s, cols, range(PACK))
            return sums

        def relu(on_scalar, sums, s, cols):
            dst = h_woven[s][:, cols, :].rearrange("p (c i) t -> p c t i", i=2)
            src = sums[:].rearrange("p t (c i) -> p c t i", i=2)
            if on_scalar:
                nc.scalar.activation(dst, src, RELU)
            else:
                nc.vector.tensor_scalar_max(dst, src, 0.0)

        def quantize_h(s, cols):
            quantize(h_codes[s][:, cols], h_scales[s][:, cols], h_woven[s][:, cols, :])

        def second(dst, b, s, cols):
            product(dst, w2_codes[b][:], w2_scales[b][:], h_codes[s][:, cols], h_scales[s][:, cols])

        whole, left, right = slice(0, SLICE), slice(0, P), slice(P, SLICE)

        relu(True, first(0, 0, left), 0, left)
        relu(False, first(1, 0, right), 0, right)
        relu(True, first(2, 1, left), 1, left)
        quantize_h(0, left)
        quantize_h(0, right)
        relu(True, first(3, 1, right), 1, right)
        quantize_h(1, left)
        relu(False, first(4, 2, left), 2, left)
        relu(True, first(5, 2, right), 2, right)
        quantize_h(1, right)
        quantize_h(2, left)
        quantize_h(2, right)

        y = [sb([P, S], F32, name) for name in ("y0", "h_woven2")]

        def leave(engine, number, b, parts):
            width = sum(cols.stop - cols.start for s, cols in parts)
            sums = bank(number, [width])
            at = 0
            for s, cols in parts:
                second(sums[:, at : at + cols.stop - cols.start], b, s, cols)
                at = at + cols.stop - cols.start
            start = parts[0][0] * SLICE + parts[0][1].start
            engine(y[b][:, start : start + width], sums[:])

        leave(nc.scalar.copy, 6, 0, [(0, whole)])
        leave(nc.scalar.copy, 0, 0, [(1, whole)])
        leave(nc.vector.tensor_copy, 7, 1, [(0, whole), (1, whole)])
        leave(nc.scalar.copy, 2, 0, [(2, left)])
        leave(nc.scalar.copy, 3, 0, [(2, right)])
        leave(nc.scalar.copy, 5, 1, [(2, whole)])

        pieces = [slice(c * P, (c + 1) * P) for c in range(PIECES)]
        gated = [sb([P, V], F32, f"gated{d}") for d in range(D)]
        gated_last = sb([P, V], F32, "gated_last")
        plain = [sb([P, V], F32, f"plain{d}") for d in range(PLAIN)]
        scaled = [sb([P, V], F32, f"scaled{d}") for d in range(PLAIN)]
        summed = sb([P, V], F32, "summed")
        result = [sb([P, V], F32, f"result{b}") for b in range(2)]

        def fetch_gated(dst, b, d, cols=slice(0, V)):
            nc.vector.tensor_tensor(dst[:, cols], y[b][:].indirect(places(pos_sb[d], cols)), gates[:, d, cols], MULT)

        def flip(dst, src, start, stop):
            nc.tensor.matmul(dst, src, identity[:], start=start, stop=stop, is_transpose=True)

        def finish(b, back, last_turn, cols):
            nc.vector.tensor_tensor(result[b][:, cols], back, last_turn[:, cols], ADD)
            nc.sync.dma_start(out=out[b * P : (b + 1) * P, cols], in_=result[b][:, cols])

        sums0 = bank(4, [V])
        turned = [bank(number, [V]) for number in (6, 7, 5)]
        for d in range(2):
            fetch_gated(gated[d], 0, d)
            for c in range(PIECES):
                flip(sums0[:, pieces[c]], gated[d][:, pieces[c]], (d, c) == (0, 0), (d, c) == (1, PIECES - 1))
        for d in range(PLAIN):
            nc.scalar.activation(plain[d][:], y[1][:].indirect(pos_sb[d][:]), COPY)
            for c in range(PIECES):
                flip(turned[d][:, pieces[c]], plain[d][:, pieces[c]], True, True)
        for d in range(2, D):
            fetch_gated(gated[d], 0, d)
        fetch_gated(gated_last, 1, 3, slice(0, 2 * P))
        pair = sb([P, V], F32, "pair")
        nc.vector.tensor_tensor(pair[:], gated[2][:], gated[3][:], ADD)
        fetch_gated(gated_last, 1, 3, slice(2 * P, V))

        def scale(d, c):
            nc.scalar.activation(scaled[d][:, pieces[c]], turned[d][:, pieces[c]], COPY, scale=gate_cols[:, d, c : c + 1])

        nc.scalar.copy(summed[:], sums0[:])
        for c in range(PIECES):
            scale(0, c)
        back0 = bank(0, [V])
        back1 = [bank(1 + c, [P]) for c in range(PIECES)]
        for c in range(PIECES):
            flip(back0[:, pieces[c]], summed[:, pieces[c]], True, True)
        for c in range(PIECES):
            flip(back1[c][:], scaled[0][:, pieces[c]], True, False)
        for cols in (pieces[0], slice(P, V)):
            finish(0, back0[:, cols], pair, cols)
        for c in range(PIECES):
            for d in range(1, PLAIN):
                scale(d, c)
                flip(back1[c][:], scaled[d][:, pieces[c]], False, d == PLAIN - 1)
            finish(1, back1[c][:], gated_last, pieces[c])
